import numpy as np, ml_dtypes
CORES = [48,51,52,55]
N = 4
BF = ml_dtypes.bfloat16
W, K, E, TH, ST, RO = 8192, 256, 32, 9, 1, 6
def subset(rng, cnt):
    a = 2 * rng.integers(0, 8, cnt.shape) + 1; o = rng.integers(0, 16, cnt.shape)
    return (((a * np.arange(16)[:, None] + o) & 15) < cnt).astype(np.int16)
def parts(rng):
    x = rng.integers(0, 256, (N, 8, 1, W), dtype=np.int16) + rng.integers(-12, 13, (N, 8, 16, W), dtype=np.int16)
    x = np.where(rng.random((N, 8, 1, W)) < 0.125, rng.integers(0, 256, (N, 8, 16, W), dtype=np.int16), np.clip(x, 0, 255))
    stk = rng.integers(0, W, (N, 8, 16, K)); bas = rng.integers(0, W, (N, 8, 16, K)); con = rng.integers(0, W, (N, 8, 16, K)); ln = rng.integers(1, 16, (N, 8, K))
    lv = (255.0 * (1.0 - rng.random((N, 8, 1, K)) ** 2)).astype(np.int64)
    z = np.clip(lv + rng.integers(-12, 13, (N, 8, 16, K)), 0, 255); w = rng.integers(1, 258, (N, 8, 16, 1))
    return x, stk, bas, con, ln, z, w
def pack(x, stk, bas, con, ln, z, w):
    def t(a, n): return np.ascontiguousarray(np.reshape(a, (N, 128, n)))
    return {"xt": t(x, W).astype(np.float32).astype(BF), "stk": t(stk, K).astype(np.int32), "bas": t(bas, K).astype(np.int32), "con": t(con, K).astype(np.int32),
            "ln": np.ascontiguousarray(ln).astype(np.int32), "z": t(z, K).astype(np.float32).astype(BF), "w": t(w, 1).astype(np.int32)}
def setup_inputs(rng):
    return pack(*parts(rng))
def setup_inputs_spread(rng):
    x, stk, bas, con, ln, z, w = parts(rng)
    x = (np.exp2(8.0 * rng.random((N, 8, 1, W), dtype=np.float32)) * rng.random((N, 8, 16, W), dtype=np.float32)).astype(np.int16)
    x = np.minimum(x, 255) * (rng.random((N, 8, 1, W)) > 0.0625)
    z = np.minimum((np.exp2(8.0 * rng.random((N, 8, 1, K))) * rng.random((N, 8, 16, K))).astype(np.int64), 255)
    def skew(lo, n, shape):
        e = rng.choice(np.array([0.25, 1.0, 4.0]), (N, 8) + (1,) * (len(shape) - 2))
        return np.minimum(lo + (n * rng.random(shape) ** e).astype(np.int64), lo + n - 1)
    stk = skew(0, W, (N, 8, 16, K)); bas = skew(0, W, (N, 8, 16, K)); con = skew(0, W, (N, 8, 16, K)); ln = skew(1, 15, (N, 8, K))
    w = np.minimum(np.exp2(8.01 * rng.random((N, 8, 16, 1))).astype(np.int64), 257)
    return pack(x, stk, bas, con, ln, z, w)
def endnames(rng):
    a = (W - 1) * rng.integers(0, 2, (N, 8, 16, K))
    s = (W - 1) * ((np.arange(16)[:, None] >= rng.integers(0, 17, (N, 8, 1, K))).astype(np.int64) ^ rng.integers(0, 2, (N, 8, 1, K)))
    ty = rng.random((N, 8, 1, K))
    return np.where(ty < 0.4, a, np.where(ty < 0.75, s, rng.integers(0, W, (N, 8, 16, K))))
def setup_inputs_ends(rng):
    cnt = rng.choice(np.array([0, 1, TH - 2, TH - 1, TH, 12, 16]), (N, 8, 1, W)); cnt[1] = np.minimum(cnt[1], TH - 2)
    x = 255 * subset(rng, cnt)
    zc = rng.choice(np.array([0, 1, 3, TH - 1, TH, 12]), (N, 8, 1, K)); zc[0] = rng.choice(np.array([TH, 12, 15]), (8, 1, K)); zc[1] = 1
    z = 255 * (1 - subset(rng, zc)); stk = endnames(rng); bas = endnames(rng); con = endnames(rng)
    for k in (0, K // 2, K - 1): z[1, 0, :, k] = 0
    ln = 1 + 14 * rng.integers(0, 2, (N, 8, K)); w = 1 + 256 * rng.integers(0, 2, (N, 8, 16, 1)); q = N - 1
    w[q, 7] = 257; w[q, 0] = 1; w[q, 6, 0] = 257; x[q, 6:8, :, 0] = 0; x[q, 7, :, W - 1] = 255; x[q, 6, :, W - 1] = 0; x[q, 6, 0, W - 1] = 255
    for k in (0, K - 1): stk[q, 7, :, k] = 0; stk[q, 7, 15, k] = W - 1
    for k in (1, K - 2): stk[q, 7, :, k] = W - 1
    for k in (2, K - 3): stk[q, 7, :, k] = 0; stk[q, 7, 0, k] = W - 1
    for k in (0, 1, 2, K - 3, K - 2, K - 1): z[q, 7, :, k] = 255
    for k in (2, K - 1): stk[q, 6, :, k] = W - 1; z[q, 6, :12, k] = 0; z[q, 6, 12:, k] = 255
    return pack(x, stk, bas, con, ln, z, w)
def setup_inputs_corners(rng):
    x, stk, bas, con, ln, z, w = parts(rng)
    cnt = rng.choice(np.array([0, TH - 1, TH, 16]), (N, 8, 1, W))
    over = rng.integers(0, 2, (N, 8, 1, W), dtype=np.int16) * rng.integers(0, 56, (N, 8, 16, W), dtype=np.int16)
    x = np.where(subset(rng, cnt) > 0, 200 + over, rng.integers(0, 200, (N, 8, 16, W), dtype=np.int16))
    z[:] = np.where(rng.random((N, 8, 1, K)) < 0.125, 201, 200); i = np.arange(16)[:, None]
    for q in range(N):
        for g in range(8):
            hot = np.flatnonzero(cnt[q, g, 0] >= TH); cold = np.flatnonzero(cnt[q, g, 0] < TH)
            row = rng.integers(1, 17, K); row[0] = 1; row[1] = 16; row[2] = 14; row[K - 1] = 15; row[K - 2] = 16
            hn = hot[rng.integers(0, len(hot), (16, K))]; cn = cold[rng.integers(0, len(cold), (16, K))]
            stk[q, g] = np.where(i == row, hn, np.where(i > row, stk[q, g], np.where((i == 0) & (rng.random((1, K)) < 0.5), hn, cn)))
    ln = rng.choice(np.array([1, 2, 14, 15]), (N, 8, K))
    for q in range(N): ln[q, q % 8] = 15; ln[q, (q + 1) % 8] = 1
    four = np.arange(K) % 4; stk[:, 3] = stk[:, 3][..., four]; z[:, 3] = z[:, 3][..., four]
    bas[:, 4] = (W - 1) * rng.integers(0, 2, (N, 16, K)); con[:, 2] = (W - 1) * rng.integers(0, 2, (N, 16, K))
    stk[:, 5] = stk[:, 5, :1].copy(); stk[:, 6] = E * np.arange(K) + rng.integers(0, E, (N, 16, K)); bas[:, 6] = E * np.arange(K) + rng.integers(0, E, (N, 16, K))
    w[0] = 1; w[N - 1] = 257
    return pack(x, stk, bas, con, ln, z, w)
def setup_inputs_long(rng):
    x, stk, bas, con, ln, z, w = parts(rng)
    x = np.where(rng.random((N, 8, 1, W)) < 0.06, rng.integers(250, 254, (N, 8, 16, W), dtype=np.int16), np.minimum(x, 249))
    ty = rng.random((N, 8, 1, K)); z = np.where(ty < 0.4, 250, np.where(ty < 0.8, 254, z)); ln = np.maximum(ln, rng.integers(1, 16, (N, 8, K)))
    return pack(x, stk, bas, con, ln, z, w)
def setup_inputs_alike(rng):
    x, stk, bas, con, ln, z, w = parts(rng); ga, gb, gc = [int(g) for g in rng.permutation(8)[:3]]; o = int(rng.integers(0, N))
    for a in (stk, bas, con):
        a[:, gb] = np.where(rng.random((N, 16, K)) < 0.5, E * rng.integers(K - 16, K, (N, 16, K)) + E - 1, a[:, gb])
    w[:, gb] = E * rng.integers(1, 256 // E + 1, (N, 16, 1)); w[:, gb, 0] = 1 + 256 * rng.integers(0, 2, (N, 1))
    for i in range(N):
        q = (o + i * ST) % N; lo, hi = ((32, 63), (96, 127), (192, 254), (96, 127), (0, 255))[min(i, 4)]
        if i < 4:
            x[q] = rng.integers(lo, hi + 1, (8, 16, W)); z[q] = 255 if i == 1 else 0
        if i == 2:
            m = np.zeros(8 * K, dtype=bool); m[rng.permutation(8 * K)[:K * int(rng.integers(0, 8)) + int(rng.integers(1, K))]] = True
            z[q] = np.where(m.reshape(8, 1, K), 255, 0)
        for g, v in ((ga, int(rng.integers(1, 4))), (gc, 0)):
            one = rng.integers(lo, hi - 2, 16); one[15] += (v - int(np.sum(one))) % 4
            x[q, g] = one[:, None]
        x[q, gb, 0] = (hi + 1) // E * E - 1
    return pack(x, stk, bas, con, ln, z, w)
def check_inputs(d):
    bad = []
    for k, lo, hi in (("xt", 0, 255), ("stk", 0, W - 1), ("bas", 0, W - 1), ("con", 0, W - 1), ("ln", 1, 15), ("z", 0, 255), ("w", 1, 257)):
        v = np.asarray(d[k]).astype(np.float32)
        if not (np.min(v) >= lo and np.max(v) <= hi and np.all(v == np.floor(v))): bad.append("range of " + k)
    return bad
def reference(xt, stk, bas, con, ln, z, w):
    X = xt.astype(np.float32).astype(np.int32).reshape(N, 8, 16, W); Z = z.astype(np.float32).astype(np.int64).reshape(N, 8, 16, K); wt = w.astype(np.int64).reshape(N, 8, 16, 1)
    S = stk.astype(np.int64).reshape(N, 8, 16, K); B = bas.astype(np.int64).reshape(N, 8, 16, K); C = con.astype(np.int64).reshape(N, 8, 16, K); n = ln.astype(np.int64).reshape(N, 8, K)
    A = [0] * N; p = np.arange(16)[None, :, None]
    for t in range(RO):
        for q in range(N):
            b = (q - t * ST) % N
            s, zz = S[b].copy(), Z[b].copy()
            R = np.take_along_axis(X[q], s.reshape(8, 1, 16 * K), 2).reshape(8, 16, 16, K).astype(np.int64)
            votes = np.add.reduce((R >= zz[:, :, None, :]).astype(np.int64), axis=1)
            hit = votes >= TH; hit[:, 0] = False
            found = np.maximum.accumulate(hit.astype(np.int64), axis=1)
            handled = found[:, 15] == 1; h = 16 - np.add.reduce(found, axis=1)
            M = np.max(np.where(found[:, None] == 1, 0, R), axis=2)
            u = np.add.reduce(wt[q] * M, axis=1) & 4095
            xh = np.take_along_axis(R, np.minimum(h, 15)[:, None, None, :], 2)[:, :, 0]
            v = np.add.reduce(xh, axis=1) & 3
            j = (((u * u) >> 5) + u + A[q]) & (K - 1)
            paste = handled & (v > 0)
            m = np.where(paste, np.take_along_axis(n[q], j, 1), 0)
            src = p + (np.where(paste, h + 1, h) - m)[:, None, :]
            low = np.take_along_axis(s, np.clip(src, 0, 15), 1); piece = np.take_along_axis(C[q], j[:, None, :], 2)
            new = np.where(p < m[:, None, :], piece, np.where(src <= 15, low, B[b]))
            S[b] = np.where(handled[:, None, :], new, s)
            Z[b] = np.where(handled[:, None, :], np.abs(xh - zz), M)
            C[q] = np.where(paste[:, None, :] & (p < h[:, None, :]), s, C[q])
            n[q] = np.where(paste, h, n[q])
            A[q] = int(np.sum(np.where(handled, 0, 1)))
            if t < RO - 1:
                col = (E * np.arange(K) + (u & (E - 1)))[:, None, :]
                np.put_along_axis(X[q], col, ((np.take_along_axis(X[q], col, 2) + M) >> 1).astype(np.int32), 2)
    last = [(q - (RO - 1) * ST) % N for q in range(N)]
    return {"ys": S[last].reshape(N, 128, K).astype(np.float32), "yc": C.reshape(N, 128, K).astype(np.float32), "yn": n.astype(np.float32), "yz": Z[last].reshape(N, 128, K).astype(np.float32).astype(BF)}

@@ -1,0 +1,521 @@
+import math
+from concourse.bass import DstId, RemoteDMATransfer
+from concourse.mybir import AluOpType as OP, AxisListType, ActivationFunctionType as AF
+
+RO = 6
+CH, L = 2, 128
+K = CH * L
+PIECES = [(0, 64, "V"), (64, 64, "A"), (128, 64, "A"), (192, 64, "A")]
+CHUNKS = [(0, 128, 0), (128, 64, 0), (192, 64, 0)]
+SIGNQ = 1
+DELTA = 100.0
+
+SCRATCH = {
+    "XT": ("sbuf", [128, 8192], "bfloat16"), "PC": ("sbuf", [128, 2048], "float32"),
+    "NB0": ("sbuf", [128, 256], "bfloat16"), "NB1": ("sbuf", [128, 256], "bfloat16"),
+    "EALL": ("sbuf", [128, 2048], "bfloat16"), "RALL": ("sbuf", [128, 2048], "bfloat16"), "RESET": ("sbuf", [128, 2048], "bfloat16"),
+    "BO": ("sbuf", [128, 128], "bfloat16"), "IDM": ("sbuf", [128, 128], "bfloat16"), "NID": ("sbuf", [128, 128], "bfloat16"),
+    "ONES": ("sbuf", [128, 128], "bfloat16"), "DIAG": ("sbuf", [128, 512], "bfloat16"), "WE": ("sbuf", [128, 128], "bfloat16"),
+    "WO": ("sbuf", [128, 128], "bfloat16"), "T1": ("sbuf", [128, 16], "bfloat16"), "T2": ("sbuf", [128, 32], "bfloat16"),
+    "NV": ("sbuf", [128, 128], "float32"), "SEL": ("sbuf", [128, 128], "bfloat16"),
+    "IO1": ("sbuf", [128, 2048], "bfloat16"), "IO2": ("sbuf", [128, 128], "bfloat16"), "IO3": ("sbuf", [128, 2048], "bfloat16"),
+    "IO4": ("sbuf", [128, 128], "bfloat16"), "IO5": ("sbuf", [128, 128], "int32"), "RL1": ("sbuf", [128, 128], "int32"),
+    "RL2": ("sbuf", [128, 128], "int32"), "RLU": ("sbuf", [128, 128], "uint16"), "K0": ("sbuf", [128, 16], "int32"),
+    "KT": ("sbuf", [128, 16], "int32"), "KM": ("sbuf", [128, 16], "int32"), "K32": ("sbuf", [128, 16], "int32"),
+    "PI": ("sbuf", [128, 8], "int32"), "PF": ("sbuf", [128, 24], "float32"), "F4": ("sbuf", [128, 16], "float32"),
+    "Z0": ("sbuf", [128, 16], "float32"), "PWS": ("sbuf", [128, 16], "float32"), "PWM": ("sbuf", [128, 16], "float32"),
+    "PW": ("sbuf", [128, 1], "float32"), "WI": ("sbuf", [128, 8], "int32"), "WF": ("sbuf", [128, 8], "float32"),
+    "LNI": ("sbuf", [128, 256], "int32"), "LNB": ("sbuf", [128, 256], "bfloat16"), "PCM": ("sbuf", [128, 256], "bfloat16"),
+    "STI": ("sbuf", [128, 256], "int32"), "BAI": ("sbuf", [128, 256], "int32"), "COI": ("sbuf", [128, 256], "int32"),
+    "HD": ("sbuf", [128, 16], "bfloat16"), "AR": ("sbuf", [128, 1], "float32"), "AC": ("sbuf", [128, 1], "float32"),
+    "FI": ("sbuf", [128, 256], "int32"), "FJ": ("sbuf", [128, 256], "int32"), "FC": ("sbuf", [128, 256], "float32"),
+    "FN": ("sbuf", [128, 256], "int32"), "FM": ("sbuf", [128, 256], "int32"), "FL": ("sbuf", [128, 256], "float32"),
+    "YSF": ("sbuf", [128, 256], "float32"),
+    "RP": ("sbuf", [128, 8192], "bfloat16"),
+    "GE": ("sbuf", [128, 4096], "bfloat16"), "WR": ("sbuf", [128, 4096], "float32"), "HP": ("sbuf", [128, 256], "bfloat16"),
+    "ZH": ("sbuf", [128, 256], "bfloat16"), "DA": ("sbuf", [128, 512], "float32"), "DB": ("sbuf", [128, 512], "float32"),
+    "SM": ("sbuf", [128, 512], "int32"), "SF": ("sbuf", [128, 32], "float32"), "LU": ("sbuf", [128, 128], "uint16"),
+    "ME": ("sbuf", [128, 256], "bfloat16"), "YE": ("sbuf", [128, 256], "bfloat16"), "XS": ("sbuf", [128, 256], "int32"),
+    "XD": ("sbuf", [128, 256], "int32"), "AB": ("sbuf", [128, 256], "float32"), "AD": ("sbuf", [128, 256], "float32"),
+    "QQ": ("sbuf", [128, 256], "int32"), "SI": ("sbuf", [128, 256], "int32"), "S8": ("sbuf", [128, 256], "float32"),
+    "MD": ("sbuf", [128, 256], "bfloat16"), "ML": ("sbuf", [128, 256], "bfloat16"), "PL": ("sbuf", [128, 256], "float32"),
+    "pz": ("psum", [128, 512], "float32"), "pva": ("psum", [128, 512], "float32"), "pvb": ("psum", [128, 512], "float32"),
+    "pu": ("psum", [128, 512], "float32"), "pm": ("psum", [128, 512], "float32"), "pr0": ("psum", [128, 512], "float32"),
+    "pr1": ("psum", [128, 512], "float32"), "py": ("psum", [128, 512], "float32"),
+}
+for _d in range(4):
+    SCRATCH["BB%d" % _d] = ("sbuf", [128, 256], "float32")
+for _n, _ty in (("U", "uint16"), ("Z", "bfloat16"), ("H", "bfloat16"), ("L", "bfloat16")):
+    SCRATCH["S" + _n] = ("sbuf", [128, RO * 256], _ty)
+    SCRATCH["O" + _n] = ("sbuf", [128, 2 * 256], _ty)
+
+SEMAPHORES = ["cV", "cA", "cT", "cG", "loc"] + ["lo%d" % i for i in range(20)] + ["dm%d" % i for i in range(24)] + ["bs%d" % d for d in (1, 2, 3)] + \
+             ["ar%d%d%s" % (t, c, s) for t in range(1, RO) for c in range(CH) for s in "ab"]
+
+ORDER = {}
+BONUS = {"vy": 8000.0, "v": 1000.0, "AC": -4000.0, "h": -4000.0, "AB": 4000.0, "IO": -20000.0, "pu": -1000.0, "XS": 4000.0, "u": 4000.0, "MD": 4000.0}
+CYC = 0.83 * 1.2
+G_R = 1.55
+
+
+def make_order(ops, deps, log=None):
+    n = len(ops)
+    succ = [[] for _ in range(n)]
+    for i in range(n):
+        for j in deps[i]:
+            succ[j].append(i)
+    prio = [0.0] * n
+    for i in range(n - 1, -1, -1):
+        op = ops[i]
+        prio[i] = op["cost"] + max([op["lat"] + prio[x] for x in succ[i]] + [0.0])
+    for i in range(n):
+        prio[i] += max([BONUS.get(w.split(":")[0].rstrip("0123456789"), 0.0) for w in ops[i]["w"]] + [-9e9]) if ops[i]["w"] else 0.0
+    left = [len(deps[i]) for i in range(n)]
+    est = [0.0] * n
+    qs = ["V", "A", "T", "S", "G"]
+    ready = {q: [] for q in qs}
+    for i in range(n):
+        if left[i] == 0:
+            ready[ops[i]["q"]].append(i)
+    qt = {q: 0.0 for q in qs}
+    order = []
+    while len(order) < n:
+        best = None
+        for q in qs:
+            if not ready[q]:
+                continue
+            m0 = max(qt[q], min([est[i] for i in ready[q]]))
+            if best is None or m0 < best[0]:
+                best = (m0, q)
+        m0, q = best
+        i = max([x for x in ready[q] if est[x] <= m0 + DELTA], key=lambda x: (prio[x], -x))
+        st = max(qt[q], est[i])
+        ready[q].remove(i)
+        qt[q] = st + ops[i]["cost"]
+        order.append(i)
+        if log is not None:
+            log.append((i, st))
+        for x in succ[i]:
+            cross = ops[x]["q"] != q or deps[x][i]
+            est[x] = max(est[x], qt[q] + (ops[i]["lat"] if cross else 0.0))
+            left[x] -= 1
+            if left[x] == 0:
+                ready[ops[x]["q"]].append(x)
+    return order, max(qt.values())
+
+
+def rank_program(g, core, T, topo):
+    rank = T.rank_of(core)
+    if rank is None:
+        return
+    n_ranks = len(T.cores)
+    ops = []
+    eng = {"V": g.vector, "A": g.scalar, "T": g.tensor, "S": g.sync, "G": g}
+
+    def add(q, fns, reads, writes, cost, lat=60.0, kind="c", sem=None, amount=0, banks=()):
+        ops.append({"q": q, "fns": fns if isinstance(fns, list) else [fns], "r": list(reads), "w": list(writes), "cost": cost,
+                    "lat": lat, "kind": kind, "sem": sem, "amount": amount, "banks": list(banks)})
+
+    def vc(n, rate=1.0):
+        return max(64.0, n * rate) * CYC
+
+    def isps(keys):
+        return sorted(set(k.split(":")[0] for k in keys if k.startswith("p")))
+
+    def V(fn, reads, writes, n, rate=1.0):
+        add("V", fn, reads, writes, vc(n, rate), banks=isps(list(reads) + list(writes)))
+
+    def A(fn, reads, writes, n, rate=1.0, extra=0.0):
+        add("A", fn, reads, writes, vc(n, rate) + extra, banks=isps(list(reads) + list(writes)))
+
+    def P(fns, reads, writes, cyc):
+        add("T", fns, reads, writes, cyc * 0.8, banks=isps(list(reads) + list(writes)))
+
+    def G(fn, reads, writes, n):
+        add("G", fn, reads, writes, 130 + 2 * n * CYC)
+
+    ndma = [0]
+
+    def D(q, fn, reads, writes, lat=2500.0):
+        add(q, fn, reads, writes, 60.0, lat, "d", "dm%d" % ndma[0], 16)
+        ndma[0] += 1
+
+    v, s, te = g.vector, g.scalar, g.tensor
+
+    def tt(o, a, b, op):
+        return lambda: v.tensor_tensor(out=o, in0=a, in1=b, op=op)
+
+    def ts(o, a, s1, op0, s2=None, op1=None):
+        if op1 is None:
+            return lambda: v.tensor_scalar(out=o, in0=a, scalar1=s1, scalar2=None, op0=op0)
+        return lambda: v.tensor_scalar(out=o, in0=a, scalar1=s1, scalar2=s2, op0=op0, op1=op1)
+
+    def cp(o, a):
+        return lambda: v.tensor_copy(out=o, in_=a)
+
+    def scan(o, d0, d1, op1, ini=0.0):
+        return lambda: v.tensor_tensor_scan(out=o, data0=d0, data1=d1, initial=ini, op0=OP.mult, op1=op1)
+
+    def act(o, a, f, bias=0.0):
+        return lambda: s.activation(out=o, in_=a, func=f, bias=bias)
+
+    def mm(o, lh, rh, st, sp):
+        return lambda: te.matmul(out=o, lhsT=lh, rhs=rh, start=st, stop=sp)
+
+    def ms(o, x):
+        return lambda: v.memset(o, x)
+
+    def io(o, pat, ch, flag=True, base=0):
+        if flag:
+            return lambda: g.iota(o, pattern=pat, base=base, channel_multiplier=ch, allow_small_or_imprecise_dtypes=True)
+        return lambda: g.iota(o, pattern=pat, base=base, channel_multiplier=ch)
+
+    def dma(q, o, a):
+        return lambda: eng[q].dma_start(out=o, in_=a)
+
+    V(ms(T.PF[:, 9:10], 0.5), [], ["PF9"], 1)
+    V(ms(T.PF[:, 10:11], 64.0), [], ["PF10"], 1)
+    V(ms(T.PF[:, 11:12], 8.5), [], ["PF11"], 1)
+    for t in range(RO):
+        V(ms(T.PF[:, 16 + t:17 + t], 8192.0 * (t + 2)), [], ["PF%d" % (16 + t)], 1)
+
+    D("S", dma("S", T.XT[:], T.xt[:]), [], ["XT"], 9000.0)
+    D("A", dma("A", T.STI[:], T.stk[:]), [], ["STI"])
+    D("A", dma("A", T.SZ[:, 0:256], T.z[:]), [], ["ZZ0:0", "ZZ0:1"])
+    D("S", dma("S", T.WI[:, 0:1], T.w[:]), [], ["WI"])
+    D("S", dma("S", T.BAI[:], T.bas[:]), [], ["BAI"])
+    D("A", dma("A", T.LNI[0:8, :], T.ln[:]), [], ["LNI"])
+    D("S", dma("S", T.COI[:], T.con[:]), [], ["COI"])
+
+    G(io(T.PI[:, 0:1], [[0, 1]], 1, False), [], ["PI0"], 1)
+    V(ts(T.PI[:, 1:2], T.PI[:, 0:1], 15, OP.bitwise_and), ["PI0"], ["PI1"], 1)
+    V(ts(T.PI[:, 2:3], T.PI[:, 0:1], 112, OP.bitwise_and), ["PI0"], ["PI2"], 1)
+    V(cp(T.PF[:, 0:3], T.PI[:, 0:3]), ["PI0", "PI1", "PI2"], ["PF0"], 3)
+    pf, pmf, p16 = T.PF[:, 0:1], T.PF[:, 1:2], T.PF[:, 2:3]
+    V(ts(T.PF[:, 3:4], pmf, -1.0, OP.mult, 16.0, OP.add), ["PF0"], ["PF3"], 1)
+    V(ts(T.PF[:, 4:5], pmf, -1.0, OP.mult, 15.0, OP.add), ["PF0"], ["PF4"], 1)
+    V(ts(T.PF[:, 5:6], pf, 16.0, OP.mult), ["PF0"], ["PF5"], 1)
+    V(ts(T.PF[:, 6:7], pmf, 256.0, OP.mult), ["PF0"], ["PF6"], 1)
+    V(ts(T.PF[:, 7:8], pmf, 15.5 - 4 * SIGNQ, OP.is_gt, -7.5, OP.mult), ["PF0"], ["PF7"], 1)
+    V(ts(T.PF[:, 8:9], T.PF[:, 7:8], 8.5, OP.add), ["PF7"], ["PF8"], 1)
+    G(io(T.IO4[:], [[1, 128]], 0), [], ["IO4"], 128)
+    G(io(T.RL1[:], [[1, 16], [0, 8]], 1, False), [], ["RL1"], 128)
+    G(io(T.IO5[:], [[0, 16], [16, 8]], 0, False), [], ["IO5"], 128)
+    G(io(T.IO3[:], [[0, 128], [1, 16]], 0), [], ["IO3"], 2048)
+    G(io(T.IO1[:], [[-1, 16], [1, 128]], 0), [], ["IO1"], 2048)
+    G(io(T.IO2[:], [[16, 8], [0, 16]], 0), [], ["IO2"], 128)
+    G(io(T.K0[:], [[16, 16]], 0, False), [], ["K0"], 16)
+    G(io(T.NV[:], [[8192, 8], [256, 16]], 0, True, -256), [], ["NV"], 128)
+    V(ms(T.NV[:, 0:128:16], 0.0), [], ["NV"], 8)
+    V(ts(T.IDM[:], T.IO4[:], pf, OP.is_equal), ["IO4", "PF0"], ["IDM"], 128, .5)
+    V(ts(T.NID[:], T.IDM[:], -1.0, OP.mult), ["IDM"], ["NID"], 128, .5)
+    V(cp(T.SU[:, 0:K], T.STI[:]), ["STI"], ["SU0:0", "SU0:1"], K)
+    V(cp(T.SH[:, 0:K], T.STI[:]), ["STI"], ["HI0:0", "HI0:1"], K)
+    V(tt(T.SL[:, 0:K], T.STI[:], T.SH[:, 0:K], OP.subtract), ["STI", "HI0:0", "HI0:1"], ["LO0:0", "LO0:1"], K, 2)
+    V(ts(T.RL2[:], T.RL1[:], 15, OP.bitwise_and), ["RL1"], ["RL2"], 128)
+    V(tt(T.RL1[:], T.RL2[:], T.IO5[:], OP.add), ["RL2", "IO5"], ["RL1"], 128, 2)
+    V(cp(T.RLU[:], T.RL1[:]), ["RL1"], ["RLU"], 128)
+    A(act(T.RALL[:], T.IDM[:, 0:128].indirect(T.RLU[:, 0:128]), AF.Copy), ["IDM", "RLU"], ["RALL"], 2048, G_R)
+    V(ts(T.EALL[:], T.IO1[:], p16, OP.is_equal), ["IO1", "PF0"], ["EALL"], 2048, .5)
+    V(ts(T.RESET[:], T.IO3[:], 0.5, OP.is_gt), ["IO3"], ["RESET"], 2048, .5)
+    V(ts(T.DIAG[:], T.IO3[:, 0:512], pmf, OP.is_equal), ["IO3", "PF0"], ["DIAG"], 512, .5)
+    V(ts(T.T1[:], T.IO4[:, 0:16], pmf, OP.is_gt), ["IO4", "PF0"], ["T1"], 16)
+    V(ts(T.T2[:], T.IO4[:, 0:32], T.PF[:, 3:4], OP.is_ge), ["IO4", "PF3"], ["T2"], 32)
+    V(ms(T.T2[:, 16:32], 0.0), [], ["T2"], 16)
+    V(ts(T.BO[:], T.IO2[:], p16, OP.is_equal), ["IO2", "PF0"], ["BO"], 128, .5)
+    V(ms(T.ONES[:], 1.0), [], ["ONES"], 128, .5)
+    V(ts(T.KT[:], T.K0[:], pmf, OP.add), ["K0", "PF0"], ["KT"], 16)
+    V(ts(T.KM[:], T.KT[:], 16.0, OP.mult, 4095.0, OP.add), ["KT"], ["KM"], 16)
+    V(ts(T.K32[:], T.KT[:], 32.0, OP.mult), ["KT"], ["K32"], 16)
+    V(ms(T.F4[:], 4.0), [], ["F4"], 16)
+    V(ms(T.Z0[:], 0.0), [], ["Z0"], 16)
+    V(scan(T.PWS[:], T.F4[:], T.Z0[:], OP.add, 64.0), ["F4", "Z0"], ["PWS"], 16)
+    V(ms(T.PWS[:, 15:16], 0.0), [], ["PWS"], 1)
+    V(ts(T.PWM[:], T.IO4[:, 0:16], T.PF[:, 4:5], OP.is_equal), ["IO4", "PF4"], ["PWM"], 16)
+    V(tt(T.PWM[:], T.PWM[:], T.PWS[:], OP.mult), ["PWM", "PWS"], ["PWM"], 16)
+    V(lambda: v.tensor_reduce(out=T.PW[:], in_=T.PWM[:], axis=AxisListType.X, op=OP.add), ["PWM"], ["PW"], 16)
+    V(ts(T.WI[:, 2:3], T.WI[:, 0:1], 510, OP.bitwise_and), ["WI"], ["WI2"], 1)
+    V(ts(T.WI[:, 3:4], T.WI[:, 0:1], 1, OP.bitwise_and), ["WI"], ["WI3"], 1)
+    V(cp(T.WF[:, 2:4], T.WI[:, 2:4]), ["WI2", "WI3"], ["WF"], 2)
+    V(ts(T.WE[:], T.BO[:], T.WF[:, 2:3], OP.mult), ["BO", "WF"], ["WE"], 128)
+    V(ts(T.WO[:], T.BO[:], T.WF[:, 3:4], OP.mult), ["BO", "WF"], ["WO"], 128)
+    V(ms(T.AC[:], -0.4375), [], ["AC"], 1)
+    V(ts(T.BB0[:], T.BAI[:], 8192.0, OP.add), ["BAI"], ["BB0"], 256)
+
+    def remote(pairs, dst, sem, lsem):
+        es = topo.engines(core, dst)
+        per = len(es) // len(pairs)
+        rid, pid, _ = topo.addr(dst)
+        tr = []
+        for i, (o, a) in enumerate(pairs):
+            m = sum(1 << e for e in es[i * per:(i + 1) * per])
+            tr.append(RemoteDMATransfer(dst_ids=[DstId(rid=rid, pnc=pid)], dma_engine_mask=m, remote_sem=T.sem[sem], srcs=[a], dsts=[o], alu_op=0))
+        return lambda: g.remote_dma_fused(tr, local_sem=T.sem[lsem])
+
+    n_eng = len(topo.engines(core, T.cores[(rank + 1) % n_ranks]))
+    for d in (1, 2, 3):
+        dst = T.cores[(rank + d) % n_ranks]
+        add("G", remote([(T["BB%d" % d][:], T.BB0[:])], dst, "bs%d" % d, "loc"), ["BB0"], ["BB%d" % d], 1000.0, 4000.0, "r", "bs%d" % d, n_eng)
+    V(cp(T.LNB[0:8, :], T.LNI[0:8, :]), ["LNI"], ["LNB"], 256)
+    V(ts(T.SEL[0:8, :], T.IO2[0:8, :], T.PF[0:8, 5:6], OP.is_equal, 256.0, OP.mult), ["IO2", "PF5"], ["SEL"], 128)
+    P([mm(T.pm[:, 0:256], T.SEL[0:8, :], T.LNB[0:8, :], True, True)], ["SEL", "LNB"], ["pm:0"], 256)
+    V(ts(T.NB0[:], T.pm[:, 0:256], 7936.0, OP.add), ["pm:0"], ["NB0"], 256)
+    V(ts(T.PCM[:], T.pm[:, 0:256], T.PF[:, 6:7], OP.is_gt), ["pm:0", "PF6"], ["PCM"], 256)
+    V(ms(T.PC[:, 0:256], 0.0), [], ["PC0"], 256)
+    V(ts(T.PL[:], T.COI[:], 8192.0, OP.add), ["COI"], ["PL"], 256)
+    V(tt(T.PC[:, 256:512], T.PL[:], T.PCM[:], OP.mult), ["PL", "PCM"], ["PC1"], 256, 2)
+    V(cp(T.pm[:, 256:512], T.PL[:]), ["PL"], ["pm:c"], 256)
+    CT = T.pm[:, 256:512]
+
+    rotn = [0]
+    nloc = [0]
+    nxt = T.cores[(rank + 1) % n_ranks]
+    SM, LU, DA, DB, RP, GE = T.SM, T.LU, T.DA, T.DB, T.RP, T.GE
+    pvs = [T.pva, T.pvb]
+
+    def sm(x, w=16):
+        return SM[:, x * 16:x * 16 + w]
+
+    def bank():
+        rotn[0] += 1
+        return "pr%d" % (rotn[0] % 2)
+
+    def send(pairs, t, c, part, reads, writes):
+        sem, ls = "ar%d%d%s" % (t, c, part), "lo%d" % nloc[0]
+        nloc[0] += 1
+        add("G", remote(pairs, nxt, sem, ls), reads, writes, 300.0, 2500.0, "r", sem, n_eng)
+        ops[-1]["lsem"] = ls
+
+    for t in range(RO):
+        last = t == RO - 1
+        par = t % 2
+        NB, NN, nb, nn = T["NB%d" % par], T["NB%d" % (1 - par)], "NB%d" % par, "NB%d" % (1 - par)
+        BB, bbk = T["BB%d" % (t % 4)], "BB%d" % (t % 4)
+        r0, o0 = t * K, par * K
+        su, zz, hi, lo = [["%s%d:%d" % (x, t, c) for c in range(CH)] for x in ("SU", "ZZ", "HI", "LO")]
+        ZA = T.SZ[:, r0:r0 + K]
+        for c in range(CH):
+            P([mm(T.pz[:, c * L:c * L + L], T.IDM[:], T.SZ[:, r0 + c * L:r0 + c * L + L], True, True)], ["IDM", zz[c]], ["pz:z%d" % c], L)
+        for p0, pn, pq in PIECES:
+            a, rk = r0 + p0, ["R%d" % (x // 16) for x in range(p0, p0 + pn, 16)]
+            rd = ["XT", su[p0 // L]]
+            if pq == "A":
+                A(act(RP[:, 16 * p0:16 * (p0 + pn)], T.XT[:].indirect(T.SU[:, a:a + pn]), AF.Copy), rd, rk, pn * 16, G_R, 65.0)
+            else:
+                V(cp(RP[:, 16 * p0:16 * (p0 + pn)], T.XT[:].indirect(T.SU[:, a:a + pn])), rd, rk, pn * 16, G_R)
+        for c, (c0, cn, sq) in enumerate(CHUNKS):
+            h = c0 // L
+            Z = T.SZ[:, r0 + c0:r0 + c0 + cn]
+            Rk = ["R%d" % (x // 16) for x in range(c0, c0 + cn, 16)]
+            vrows, srows = list(range(1, 16 - 4 * sq)), list(range(16 - 4 * sq, 16))
+            for qd in range(sq):
+                bk = bank()
+                i0 = 16 - 4 * (qd + 1)
+                fns = []
+                for i in range(4):
+                    ob = T[bk][:, i * cn:(i + 1) * cn]
+                    fns += [mm(ob, T.IDM[:], RP[:, 16 * c0 + i0 + i:16 * (c0 + cn):16], True, False), mm(ob, T.NID[:], Z, False, True)]
+                P(fns, ["IDM", "NID", zz[h]] + Rk, [bk + ":s"], 8 * cn)
+                A(act(GE[:, 16 * c0 + i0 * cn:16 * c0 + (i0 + 4) * cn], T[bk][:, 0:4 * cn], AF.Sign, T.PF[:, 9:10]), [bk + ":s", "PF9"],
+                  ["GE%d:%d" % (i, c) for i in range(i0, i0 + 4)], 4 * cn)
+            for i in vrows:
+                V(tt(GE[:, 16 * c0 + i * cn:16 * c0 + (i + 1) * cn], RP[:, 16 * c0 + i:16 * (c0 + cn):16], T.pz[:, c0:c0 + cn], OP.is_ge),
+                  ["pz:z%d" % h] + Rk, ["GE%d:%d" % (i, c)], cn)
+            pv, kv = pvs[h], ("pva", "pvb")[h]
+            seq = vrows + srows
+            for x, i in enumerate(seq):
+                P([mm(pv[:, c0 - h * L:c0 - h * L + cn], T.EALL[:, i * 128:(i + 1) * 128], GE[:, 16 * c0 + i * cn:16 * c0 + (i + 1) * cn], x == 0, x == len(seq) - 1)],
+                  ["EALL", "GE%d:%d" % (i, c)], [kv + ":v"], cn)
+            V(scan(RP[:, 4096 + 16 * c0:4096 + 16 * (c0 + cn)], T.RESET[:, 0:16 * cn], RP[:, 16 * c0:16 * (c0 + cn)], OP.max), Rk + ["RESET"], ["PX%d" % c], 16 * cn, .5)
+            if c0 + cn == L or c0 + cn == K:
+                V(ts(T.HP[:, h * L:h * L + L], pv[:, 0:L], T.PF[:, 8:9] if sq else T.PF[:, 11:12], OP.is_ge, T.PW[:], OP.mult), [kv + ":v", "PW", "PF8", "PF11"], ["HP%d" % h], L)
+        allR = ["R%d" % x for x in range(16)] + ["PX%d" % c for c in range(len(CHUNKS))]
+        P([mm(T.pva[:, 3 * L:3 * L + 16], T.EALL[:, i * 128:(i + 1) * 128], T.HP[:, i:K:16], i == 0, i == 15) for i in range(16)],
+          ["EALL", "HP0", "HP1"], ["pva:l"], 16 * 64)
+        A(act(T.SF[:, 0:16], T.pva[:, 3 * L:3 * L + 16], AF.Ln, T.PF[:, 10:11]), ["pva:l", "PF10"], ["SF"], 16)
+        P([mm(T.pvb[:, L:L + K], T.BO[:], T.HP[:], True, True)], ["BO", "HP0", "HP1"], ["pvb:s"], K)
+        V(tt(T.ZH[:], ZA, T.pvb[:, L:L + K], OP.min), zz + ["pvb:s"], ["ZH"], K)
+        V(ts(sm(0), T.SF[:, 0:16], -1.0 / math.log(4.0), OP.mult, 19.0, OP.add), ["SF"], ["h"], 16)
+        V(tt(sm(2), sm(0), T.KM[:], OP.add), ["h", "KM"], ["lm"], 16)
+        V(ts(sm(1), sm(0), 15.5, OP.is_lt, -4095.0, OP.mult), ["h"], ["e"], 16)
+        V(tt(sm(3), sm(2), sm(1), OP.add), ["lm", "e"], ["ly"], 16)
+        V(cp(LU[:, 0:32], sm(2, 32)), ["lm", "ly"], ["LU0"], 32)
+        A(act(T.ME[:], RP[:].indirect(LU[:, 0:16]), AF.Copy), allR + ["LU0"], ["M"], K, G_R, 65.0)
+        A(act(T.YE[:], RP[:].indirect(LU[:, 16:32]), AF.Copy), allR + ["LU0"], ["Y"], K, G_R, 65.0)
+        P([mm(T.pu[:, 0:K], T.WE[:], T.ME[:], True, False), mm(T.pu[:, 0:K], T.WO[:], T.ME[:], False, True)], ["WE", "WO", "M"], ["pu:u"], 2 * K)
+        P([mm(T.py[:, 0:16], T.EALL[:, i * 128:(i + 1) * 128], T.YE[:, i:K:16], i == 0, i == 15) for i in range(16)], ["EALL", "Y"], ["py:y"], 16 * 64)
+        V(tt(DA[:, 0:K], T.DIAG[:, 0:K], T.pu[:, 0:K], OP.mult), ["DIAG", "pu:u"], ["DA"], K)
+        V(scan(DB[:, 0:K], T.RESET[:, 0:K], DA[:, 0:K], OP.add), ["RESET", "DA"], ["DB"], K)
+        V(cp(sm(4), DB[:, 15:K:16]), ["DB"], ["uv"], 16)
+        V(ts(sm(6), sm(4), 4095, OP.bitwise_and), ["uv"], ["uvm"], 16)
+        V(cp(sm(5), T.py[:, 0:16]), ["py:y"], ["vy"], 16)
+        u, vv = sm(6), sm(5)
+        V(ts(sm(8), u, 32.0, OP.add), ["uvm"], ["u32"], 16)
+        V(tt(T.SF[:, 16:32], u, sm(8), OP.mult), ["uvm", "u32"], ["yq"], 16)
+        V(ts(sm(9), T.SF[:, 16:32], 1.0 / 32.0, OP.mult, T.AC[:], OP.add), ["yq", "AC"], ["jf"], 16)
+        V(ts(sm(11), u, 31, OP.bitwise_and), ["uvm"], ["a31"], 16)
+        V(ts(sm(12), sm(9), 255, OP.bitwise_and), ["jf"], ["j"], 16)
+        V(tt(sm(13), sm(11), T.K32[:], OP.add), ["a31", "K32"], ["a"], 16)
+        V(cp(LU[:, 32:64], sm(12, 32)), ["j", "a"], ["LU1"], 32)
+        V(tt(T.MD[:], NB[:].indirect(LU[:, 32:48]), T.DIAG[:, 0:K], OP.mult), [nb, "LU1", "DIAG"], ["MD"], K, G_R)
+        V(ts(T.HD[:], sm(0), 15.5, OP.is_lt), ["h"], ["HD"], 16)
+        V(ts(sm(17), sm(0), 256.0, OP.mult), ["h"], ["h256"], 16)
+        V(tt(sm(18), sm(17), T.KT[:], OP.add), ["h256", "KT"], ["d0"], 16)
+        V(ts(sm(14), vv, 3, OP.bitwise_and), ["vy"], ["v3"], 16)
+        V(tt(sm(15), sm(14), T.HD[:], OP.mult), ["v3", "HD"], ["vh"], 16)
+        V(ts(sm(16), sm(15), 0.5, OP.is_gt), ["vh"], ["pa"], 16)
+        V(tt(sm(27), sm(0), sm(16), OP.mult), ["h", "pa"], ["cd"], 16)
+        V(scan(T.ML[:], T.RESET[:, 0:K], T.MD[:], OP.add), ["RESET", "MD"], ["ML"], K, .5)
+        V(tt(sm(20), T.ML[:, 15:K:16], sm(16), OP.mult), ["ML", "pa"], ["mc"], 16)
+        V(tt(sm(21), sm(18), sm(20), OP.subtract), ["d0", "mc"], ["d"], 16)
+        V(ts(sm(22), sm(20), 5, OP.arith_shift_right, 0x700, OP.bitwise_and), ["mc"], ["ver"], 16)
+        V(ts(sm(24), sm(21), 4095, OP.bitwise_and), ["d"], ["lr"], 16)
+        V(ts(sm(25), sm(21), 8, OP.arith_shift_right, 31, OP.bitwise_and), ["d"], ["ls"], 16)
+        V(tt(sm(26), sm(22), sm(12), OP.add), ["ver", "j"], ["lp"], 16)
+        V(cp(LU[:, 64:128], sm(24, 64)), ["lr", "ls", "lp", "cd"], ["LU2"], 64)
+        P([mm(T.pz[:, K:2 * K], T.IDM[:], T.YE[:], True, False), mm(T.pz[:, K:2 * K], T.NID[:], T.ZH[:], False, True)], ["IDM", "NID", "Y", "ZH"], ["pz:d"], 2 * K)
+        OZ, oz = T.OZ[:, o0:o0 + K], "OZ%d" % par
+        A(act(OZ, T.pz[:, K:2 * K], AF.Abs), ["pz:d"], [oz], K)
+        for qd in range(8):
+            bk = bank()
+            for i in range(2):
+                r = qd * 2 + i
+                ob, lh = T[bk][:, i * K:(i + 1) * K], T.RALL[:, r * 128:(r + 1) * 128]
+                P([mm(ob, lh, T.SH[:, r0:r0 + K], True, False), mm(ob, lh, T.SL[:, r0:r0 + K], False, True)], ["RALL"] + hi + lo, [bk + ":%d" % i], 2 * K)
+            if qd == 0:
+                A(act(T.S8[:], T[bk][:, 0:K], AF.Identity, T.PF[:, 16 + t:17 + t]), [bk + ":0", "PF%d" % (16 + t)], ["S8"], K)
+            A(act(T.WR[:, qd * 512:(qd + 1) * 512], T[bk][:], AF.Copy), [bk + ":0", bk + ":1"], ["WR%d" % qd], 512)
+        for c in range(CH):
+            cs, oc, nc = slice(c * L, c * L + L), slice(o0 + c * L, o0 + c * L + L), slice(r0 + K + c * L, r0 + K + c * L + L)
+            ck = ":%d" % c
+            c8 = 8 * c
+
+            def ls(x):
+                return LU[:, 64 + 16 * x + c8:64 + 16 * x + c8 + 8]
+            V(tt(T.AB[:, cs], T.T2[:].indirect(ls(1)), BB[:, cs], OP.mult), ["T2", bbk, "LU2"], ["AB" + ck], L, G_R)
+            V(tt(T.AD[:, cs], T.PC[:, 0:K * (t + 2)].indirect(ls(2)), T.AB[:, cs], OP.max), ["PC%d" % x for x in range(t + 2)] + ["AB" + ck, "LU2"], ["AD" + ck], L, G_R)
+            V(tt(T.QQ[:, cs], T.WR[:].indirect(ls(0)), T.AD[:, cs], OP.max), ["WR%d" % x for x in range(8)] + ["AD" + ck, "LU2"], ["Q" + ck], L, G_R)
+            V(ts(T.SI[:, cs], T.QQ[:, cs], 8191, OP.bitwise_and), ["Q" + ck], ["SI" + ck], L)
+            if last:
+                V(cp(T.YSF[:, cs], T.SI[:, cs]), ["SI" + ck], ["YSF" + ck], L)
+                D("S", dma("S", T.ys[:, cs], T.YSF[:, cs]), ["YSF" + ck], [])
+                if c == 0:
+                    D("S", dma("S", T.yz[:], OZ), [oz], [])
+                continue
+            ou, oh, ol = ["%s%d:%d" % (x, par, c) for x in ("OU", "OH", "OL")]
+            V(cp(T.OU[:, oc], T.SI[:, cs]), ["SI" + ck], [ou], L)
+            send([(T.SU[:, nc], T.OU[:, oc]), (T.SZ[:, nc], T.OZ[:, oc])], t + 1, c, "a", [ou, oz], ["SU%d:%d" % (t + 1, c), "ZZ%d:%d" % (t + 1, c)])
+            px = T.pva[:, cs] if c == 0 else T.pvb[:, 0:L]
+            kx = "pva:v" if c == 0 else "pvb:v"
+            V(cp(px, T.SI[:, cs]), ["SI" + ck], [kx], L)
+            A(act(T.OH[:, oc], px, AF.Copy), [kx], [oh], L)
+            V(tt(T.OL[:, oc], px, T.OH[:, oc], OP.subtract), [kx, oh], [ol], L)
+            send([(T.SH[:, nc], T.OH[:, oc]), (T.SL[:, nc], T.OL[:, oc])], t + 1, c, "b", [oh, ol], ["HI%d:%d" % (t + 1, c), "LO%d:%d" % (t + 1, c)])
+        if not last:
+            V(tt(T.XS[:], T.XT[:].indirect(LU[:, 48:64]), T.ME[:], OP.add), ["XT", "LU1", "M"], ["XS"], K, G_R)
+            V(ts(T.XD[:], T.XS[:], 1, OP.arith_shift_right), ["XS"], ["XD"], K)
+            V(cp(T.XT[:].indirect(LU[:, 48:64]), T.XD[:]), ["XD", "LU1"], ["XT"], K, 4)
+            P([mm(T.pm[:, 0:16], T.ONES[:], T.HD[:], True, True)], ["ONES", "HD"], ["pm:a"], 64)
+            V(lambda: v.tensor_reduce(out=T.AR[:], in_=T.pm[:, 0:16], axis=AxisListType.X, op=OP.add), ["pm:a"], ["AR"], 16)
+            V(ts(T.AC[:], T.AR[:], -1.0, OP.mult, 2048.0 - 0.4375, OP.add), ["AR"], ["AC"], 1)
+        pk, PD = ("PL", T.PL[:]) if last else ("PC%d" % (t + 2), T.PC[:, K * (t + 2):K * (t + 3)])
+        V(tt(PD, T.T1[:].indirect(LU[:, 112:128]), T.S8[:], OP.mult), ["T1", "S8", "LU2"], [pk], K, G_R)
+        V(tt(CT, CT, PD, OP.max), ["pm:c", pk], ["pm:c"], K)
+        V(tt(NN[:], T.NV[:, 16 * (t + 2):16 * (t + 3)].indirect(LU[:, 112:128]), NB[:], OP.max), ["NV", "LU2", nb], [nn], K, G_R)
+    NF, nf = T["NB%d" % (RO % 2)], "NB%d" % (RO % 2)
+    V(cp(T.FI[:], CT), ["pm:c"], ["FI"], K)
+    V(ts(T.FJ[:], T.FI[:], 8191, OP.bitwise_and), ["FI"], ["FJ"], K)
+    V(cp(T.FC[:], T.FJ[:]), ["FJ"], ["FC"], K)
+    D("S", dma("S", T.yc[:], T.FC[:]), ["FC"], [])
+    V(cp(T.FN[:], NF[:]), [nf], ["FN"], K)
+    V(ts(T.FM[:], T.FN[:], 8, OP.arith_shift_right, 31, OP.bitwise_and), ["FN"], ["FM"], K)
+    V(ts(T.FL[:], T.FM[:], 1.0, OP.add), ["FM"], ["FL"], K)
+    D("S", dma("S", T.yn[:], T.FL[0:128:16, :]), ["FL"], [])
+
+    lastw, readers, lastb = {}, {}, {}
+    N = len(ops)
+    deps = [dict() for _ in range(N)]
+
+    def dep(i, j, wait):
+        if i != j:
+            deps[i][j] = deps[i].get(j, False) or wait
+
+    for i in range(N):
+        op = ops[i]
+        for r in op["r"]:
+            if r in lastw:
+                dep(i, lastw[r], True)
+            readers.setdefault(r, []).append(i)
+        for w in op["w"]:
+            acc = op["q"] == "T" and w.startswith("pv")
+            if w in lastw:
+                dep(i, lastw[w], not (acc and ops[lastw[w]]["q"] == "T"))
+            for j in readers.get(w, []):
+                dep(i, j, True)
+            lastw[w] = i
+            readers[w] = []
+        for b in op["banks"]:
+            if b in lastb:
+                dep(i, lastb[b], ops[lastb[b]]["q"] != op["q"])
+            lastb[b] = i
+
+    if "order" not in ORDER:
+        ORDER["order"] = make_order(ops, deps)[0]
+    order = ORDER["order"]
+
+    CN = {"V": "cV", "A": "cA", "T": "cT", "G": "cG"}
+    count = {q: 0 for q in CN}
+    known = {q: {} for q in eng}
+    done, clock = {}, {}
+    locsum = 0
+    for i in order:
+        op = ops[i]
+        q = op["q"]
+        need = {}
+        for j, wait in deps[i].items():
+            if not wait:
+                continue
+            oj = ops[j]
+            if oj["kind"] == "r" and not any(w in op["r"] or w in op["w"] for w in oj["w"]):
+                sem, val, cl = oj["lsem"], oj["amount"], {}
+            else:
+                sem, val = done[j]
+                cl = clock[j] if oj["kind"] != "r" else {}
+            if known[q].get(sem, 0) >= val:
+                continue
+            if sem not in need or need[sem][0] < val:
+                need[sem] = (val, cl)
+        for sem in sorted(need):
+            val, cl = need[sem]
+            if any(o2 != sem and need[o2][1].get(sem, 0) >= val and not (cl.get(o2, 0) >= need[o2][0]) for o2 in need):
+                continue
+            eng[q].wait_ge(T.sem[sem], int(val))
+        for sem in need:
+            val, cl = need[sem]
+            known[q][sem] = max(known[q].get(sem, 0), val)
+            for s2 in cl:
+                known[q][s2] = max(known[q].get(s2, 0), cl[s2])
+        for f in op["fns"]:
+            ins = f()
+            if op["kind"] == "c":
+                ins.then_inc(T.sem[CN[q]], 1)
+                count[q] += 1
+            elif op["kind"] == "d":
+                ins.then_inc(T.sem[op["sem"]], 16)
+        if op["kind"] == "c":
+            done[i] = (CN[q], count[q])
+        else:
+            done[i] = (op["sem"], op["amount"])
+            if op["kind"] == "r" and "lsem" not in op:
+                locsum += n_eng
+        clock[i] = dict(known[q])
+        clock[i][done[i][0]] = max(clock[i].get(done[i][0], 0), done[i][1])
+    for q in CN:
+        if count[q]:
+            g.wait_ge(T.sem[CN[q]], count[q])
+    g.wait_ge(T.sem.loc, locsum)
+    for op in ops:
+        if op["kind"] in ("d", "r") and known["G"].get(op["sem"], 0) < op["amount"]:
+            g.wait_ge(T.sem[op["sem"]], op["amount"])
+        if "lsem" in op and known["G"].get(op["lsem"], 0) < n_eng:
+            g.wait_ge(T.sem[op["lsem"]], n_eng)

@@ -5,20 +5,22 @@ from concourse.mybir import AluOpType as OP, AxisListType, ActivationFunctionTyp
 RO = 6
 CH, L = 2, 128
 K = CH * L
-PIECES = [(0, 64, "V"), (64, 64, "A"), (128, 64, "A"), (192, 64, "A")]
+NDP = 4
+PXN = 32
+PIECES = [(0, 64, "A"), (64, 32, "V"), (96, 32, "V"), (128, 64, "A"), (192, 64, "A")]
 CHUNKS = [(0, 128, 0), (128, 64, 0), (192, 64, 0)]
 SIGNQ = 1
-DELTA = 100.0
+DELTA = 300.0
 
 SCRATCH = {
     "XT": ("sbuf", [128, 8192], "bfloat16"), "PC": ("sbuf", [128, 2048], "float32"),
     "NB0": ("sbuf", [128, 256], "bfloat16"), "NB1": ("sbuf", [128, 256], "bfloat16"),
     "EALL": ("sbuf", [128, 2048], "bfloat16"), "RALL": ("sbuf", [128, 2048], "bfloat16"), "RESET": ("sbuf", [128, 2048], "bfloat16"),
     "BO": ("sbuf", [128, 128], "bfloat16"), "IDM": ("sbuf", [128, 128], "bfloat16"), "NID": ("sbuf", [128, 128], "bfloat16"),
-    "ONES": ("sbuf", [128, 128], "bfloat16"), "DIAG": ("sbuf", [128, 512], "bfloat16"), "WE": ("sbuf", [128, 128], "bfloat16"),
-    "WO": ("sbuf", [128, 128], "bfloat16"), "T1": ("sbuf", [128, 16], "bfloat16"), "T2": ("sbuf", [128, 32], "bfloat16"),
+    "ONES": ("sbuf", [128, 256], "bfloat16"), "DIAG": ("sbuf", [128, 256], "bfloat16"), "WALL": ("sbuf", [128, 2048], "float16"),
+    "ACT": ("sbuf", [128, 16], "float32"), "KF": ("sbuf", [128, 16], "float32"), "T1": ("sbuf", [128, 16], "bfloat16"), "T2": ("sbuf", [128, 32], "bfloat16"),
     "NV": ("sbuf", [128, 128], "float32"), "SEL": ("sbuf", [128, 128], "bfloat16"),
-    "IO1": ("sbuf", [128, 2048], "bfloat16"), "IO2": ("sbuf", [128, 128], "bfloat16"), "IO3": ("sbuf", [128, 2048], "bfloat16"),
+    "IO1": ("sbuf", [128, 2048], "bfloat16"), "IO2": ("sbuf", [128, 128], "bfloat16"), "IO3": ("sbuf", [128, 256], "bfloat16"),
     "IO4": ("sbuf", [128, 128], "bfloat16"), "IO5": ("sbuf", [128, 128], "int32"), "RL1": ("sbuf", [128, 128], "int32"),
     "RL2": ("sbuf", [128, 128], "int32"), "RLU": ("sbuf", [128, 128], "uint16"), "K0": ("sbuf", [128, 16], "int32"),
     "KT": ("sbuf", [128, 16], "int32"), "KM": ("sbuf", [128, 16], "int32"), "K32": ("sbuf", [128, 16], "int32"),
@@ -30,7 +32,7 @@ SCRATCH = {
     "HD": ("sbuf", [128, 16], "bfloat16"), "AR": ("sbuf", [128, 1], "float32"), "AC": ("sbuf", [128, 1], "float32"),
     "FI": ("sbuf", [128, 256], "int32"), "FJ": ("sbuf", [128, 256], "int32"), "FC": ("sbuf", [128, 256], "float32"),
     "FN": ("sbuf", [128, 256], "int32"), "FM": ("sbuf", [128, 256], "int32"), "FL": ("sbuf", [128, 256], "float32"),
-    "YSF": ("sbuf", [128, 256], "float32"),
+    "ER": ("dram", [8, 32, 256], "float32"), "YSF": ("sbuf", [128, 256], "float32"),
     "RP": ("sbuf", [128, 8192], "bfloat16"),
     "GE": ("sbuf", [128, 4096], "bfloat16"), "WR": ("sbuf", [128, 4096], "float32"), "HP": ("sbuf", [128, 256], "bfloat16"),
     "ZH": ("sbuf", [128, 256], "bfloat16"), "DA": ("sbuf", [128, 512], "float32"), "DB": ("sbuf", [128, 512], "float32"),
@@ -41,7 +43,7 @@ SCRATCH = {
     "MD": ("sbuf", [128, 256], "bfloat16"), "ML": ("sbuf", [128, 256], "bfloat16"), "PL": ("sbuf", [128, 256], "float32"),
     "pz": ("psum", [128, 512], "float32"), "pva": ("psum", [128, 512], "float32"), "pvb": ("psum", [128, 512], "float32"),
     "pu": ("psum", [128, 512], "float32"), "pm": ("psum", [128, 512], "float32"), "pr0": ("psum", [128, 512], "float32"),
-    "pr1": ("psum", [128, 512], "float32"), "py": ("psum", [128, 512], "float32"),
+    "pr1": ("psum", [128, 512], "float32"), "pr2": ("psum", [128, 512], "float32"),
 }
 for _d in range(4):
     SCRATCH["BB%d" % _d] = ("sbuf", [128, 256], "float32")
@@ -53,7 +55,8 @@ SEMAPHORES = ["cV", "cA", "cT", "cG", "loc"] + ["lo%d" % i for i in range(20)] +
              ["ar%d%d%s" % (t, c, s) for t in range(1, RO) for c in range(CH) for s in "ab"]
 
 ORDER = {}
-BONUS = {"vy": 8000.0, "v": 1000.0, "AC": -4000.0, "h": -4000.0, "AB": 4000.0, "IO": -20000.0, "pu": -1000.0, "XS": 4000.0, "u": 4000.0, "MD": 4000.0}
+BONUS = {"IO": -2000.0, "HP": 8000.0, "XS": -20000.0, "OL": -8000.0, "pa": -2000.0, "SU": -2000.0, "pr": -20000.0, "NB": -20000.0, "pm": 8000.0,
+         "uv": -8000.0, "e": -20000.0, "HI": 2000.0, "XT": -20000.0, "pz": -20000.0}
 CYC = 0.83 * 1.2
 G_R = 1.55
 
@@ -140,6 +143,10 @@ def rank_program(g, core, T, topo):
         add(q, fn, reads, writes, 60.0, lat, "d", "dm%d" % ndma[0], 16)
         ndma[0] += 1
 
+    def DS(fns, reads, writes, lat):
+        add("S", fns, reads, writes, 60.0 * len(fns), lat, "d", "dm%d" % ndma[0], 16 * len(fns))
+        ndma[0] += 1
+
     v, s, te = g.vector, g.scalar, g.tensor
 
     def tt(o, a, b, op):
@@ -176,6 +183,7 @@ def rank_program(g, core, T, topo):
     V(ms(T.PF[:, 9:10], 0.5), [], ["PF9"], 1)
     V(ms(T.PF[:, 10:11], 64.0), [], ["PF10"], 1)
     V(ms(T.PF[:, 11:12], 8.5), [], ["PF11"], 1)
+    V(ms(T.PF[:, 12:13], 2040.0 - 0.4375), [], ["PF12"], 1)
     for t in range(RO):
         V(ms(T.PF[:, 16 + t:17 + t], 8192.0 * (t + 2)), [], ["PF%d" % (16 + t)], 1)
 
@@ -201,7 +209,7 @@ def rank_program(g, core, T, topo):
     G(io(T.IO4[:], [[1, 128]], 0), [], ["IO4"], 128)
     G(io(T.RL1[:], [[1, 16], [0, 8]], 1, False), [], ["RL1"], 128)
     G(io(T.IO5[:], [[0, 16], [16, 8]], 0, False), [], ["IO5"], 128)
-    G(io(T.IO3[:], [[0, 128], [1, 16]], 0), [], ["IO3"], 2048)
+    G(io(T.IO3[:], [[0, 16], [1, 16]], 0), [], ["IO3"], 256)
     G(io(T.IO1[:], [[-1, 16], [1, 128]], 0), [], ["IO1"], 2048)
     G(io(T.IO2[:], [[16, 8], [0, 16]], 0), [], ["IO2"], 128)
     G(io(T.K0[:], [[16, 16]], 0, False), [], ["K0"], 16)
@@ -217,16 +225,18 @@ def rank_program(g, core, T, topo):
     V(cp(T.RLU[:], T.RL1[:]), ["RL1"], ["RLU"], 128)
     A(act(T.RALL[:], T.IDM[:, 0:128].indirect(T.RLU[:, 0:128]), AF.Copy), ["IDM", "RLU"], ["RALL"], 2048, G_R)
     V(ts(T.EALL[:], T.IO1[:], p16, OP.is_equal), ["IO1", "PF0"], ["EALL"], 2048, .5)
-    V(ts(T.RESET[:], T.IO3[:], 0.5, OP.is_gt), ["IO3"], ["RESET"], 2048, .5)
-    V(ts(T.DIAG[:], T.IO3[:, 0:512], pmf, OP.is_equal), ["IO3", "PF0"], ["DIAG"], 512, .5)
+    V(ms(T.RESET[:], 1.0), [], ["RESET"], 2048, .5)
+    V(ms(T.RESET[:, 0:2048:16], 0.0), [], ["RESET"], 128, .5)
+    V(ts(T.DIAG[:], T.IO3[:], pmf, OP.is_equal), ["IO3", "PF0"], ["DIAG"], 256, .5)
     V(ts(T.T1[:], T.IO4[:, 0:16], pmf, OP.is_gt), ["IO4", "PF0"], ["T1"], 16)
     V(ts(T.T2[:], T.IO4[:, 0:32], T.PF[:, 3:4], OP.is_ge), ["IO4", "PF3"], ["T2"], 32)
     V(ms(T.T2[:, 16:32], 0.0), [], ["T2"], 16)
     V(ts(T.BO[:], T.IO2[:], p16, OP.is_equal), ["IO2", "PF0"], ["BO"], 128, .5)
-    V(ms(T.ONES[:], 1.0), [], ["ONES"], 128, .5)
+    V(ms(T.ONES[:], 1.0), [], ["ONES"], 256, .5)
     V(ts(T.KT[:], T.K0[:], pmf, OP.add), ["K0", "PF0"], ["KT"], 16)
     V(ts(T.KM[:], T.KT[:], 16.0, OP.mult, 4095.0, OP.add), ["KT"], ["KM"], 16)
     V(ts(T.K32[:], T.KT[:], 32.0, OP.mult), ["KT"], ["K32"], 16)
+    V(ts(T.KF[:], T.KT[:], -16.0 * math.log(4.0), OP.mult, -(4095.0 + 19.0) * math.log(4.0), OP.add), ["KT"], ["KF"], 16)
     V(ms(T.F4[:], 4.0), [], ["F4"], 16)
     V(ms(T.Z0[:], 0.0), [], ["Z0"], 16)
     V(scan(T.PWS[:], T.F4[:], T.Z0[:], OP.add, 64.0), ["F4", "Z0"], ["PWS"], 16)
@@ -234,12 +244,9 @@ def rank_program(g, core, T, topo):
     V(ts(T.PWM[:], T.IO4[:, 0:16], T.PF[:, 4:5], OP.is_equal), ["IO4", "PF4"], ["PWM"], 16)
     V(tt(T.PWM[:], T.PWM[:], T.PWS[:], OP.mult), ["PWM", "PWS"], ["PWM"], 16)
     V(lambda: v.tensor_reduce(out=T.PW[:], in_=T.PWM[:], axis=AxisListType.X, op=OP.add), ["PWM"], ["PW"], 16)
-    V(ts(T.WI[:, 2:3], T.WI[:, 0:1], 510, OP.bitwise_and), ["WI"], ["WI2"], 1)
-    V(ts(T.WI[:, 3:4], T.WI[:, 0:1], 1, OP.bitwise_and), ["WI"], ["WI3"], 1)
-    V(cp(T.WF[:, 2:4], T.WI[:, 2:4]), ["WI2", "WI3"], ["WF"], 2)
-    V(ts(T.WE[:], T.BO[:], T.WF[:, 2:3], OP.mult), ["BO", "WF"], ["WE"], 128)
-    V(ts(T.WO[:], T.BO[:], T.WF[:, 3:4], OP.mult), ["BO", "WF"], ["WO"], 128)
-    V(ms(T.AC[:], -0.4375), [], ["AC"], 1)
+    V(cp(T.WF[:, 0:1], T.WI[:, 0:1]), ["WI"], ["WF"], 1)
+    V(ts(T.WALL[:], T.EALL[:], T.WF[:, 0:1], OP.mult), ["EALL", "WF"], ["WALL"], 2048, .5)
+    V(ms(T.AC[:], -8.4375), [], ["AC"], 1)
     V(ts(T.BB0[:], T.BAI[:], 8192.0, OP.add), ["BAI"], ["BB0"], 256)
 
     def remote(pairs, dst, sem, lsem):
@@ -278,12 +285,12 @@ def rank_program(g, core, T, topo):
 
     def bank():
         rotn[0] += 1
-        return "pr%d" % (rotn[0] % 2)
+        return "pr%d" % (rotn[0] % 3)
 
     def send(pairs, t, c, part, reads, writes):
         sem, ls = "ar%d%d%s" % (t, c, part), "lo%d" % nloc[0]
         nloc[0] += 1
-        add("G", remote(pairs, nxt, sem, ls), reads, writes, 300.0, 2500.0, "r", sem, n_eng)
+        add("G", remote(pairs, nxt, sem, ls), reads, writes, 1000.0, 2300.0, "r", sem, n_eng)
         ops[-1]["lsem"] = ls
 
     for t in range(RO):
@@ -326,10 +333,12 @@ def rank_program(g, core, T, topo):
             for x, i in enumerate(seq):
                 P([mm(pv[:, c0 - h * L:c0 - h * L + cn], T.EALL[:, i * 128:(i + 1) * 128], GE[:, 16 * c0 + i * cn:16 * c0 + (i + 1) * cn], x == 0, x == len(seq) - 1)],
                   ["EALL", "GE%d:%d" % (i, c)], [kv + ":v"], cn)
-            V(scan(RP[:, 4096 + 16 * c0:4096 + 16 * (c0 + cn)], T.RESET[:, 0:16 * cn], RP[:, 16 * c0:16 * (c0 + cn)], OP.max), Rk + ["RESET"], ["PX%d" % c], 16 * cn, .5)
+            for x0 in range(c0, c0 + cn, PXN):
+                V(scan(RP[:, 4096 + 16 * x0:4096 + 16 * (x0 + PXN)], T.RESET[:, 0:16 * PXN], RP[:, 16 * x0:16 * (x0 + PXN)], OP.max),
+                  ["R%d" % (x // 16) for x in range(x0, x0 + PXN, 16)] + ["RESET"], ["PX:%d" % x0], 16 * PXN, .5)
             if c0 + cn == L or c0 + cn == K:
                 V(ts(T.HP[:, h * L:h * L + L], pv[:, 0:L], T.PF[:, 8:9] if sq else T.PF[:, 11:12], OP.is_ge, T.PW[:], OP.mult), [kv + ":v", "PW", "PF8", "PF11"], ["HP%d" % h], L)
-        allR = ["R%d" % x for x in range(16)] + ["PX%d" % c for c in range(len(CHUNKS))]
+        allR = ["R%d" % x for x in range(16)] + ["PX:%d" % x for x in range(0, K, PXN)]
         P([mm(T.pva[:, 3 * L:3 * L + 16], T.EALL[:, i * 128:(i + 1) * 128], T.HP[:, i:K:16], i == 0, i == 15) for i in range(16)],
           ["EALL", "HP0", "HP1"], ["pva:l"], 16 * 64)
         A(act(T.SF[:, 0:16], T.pva[:, 3 * L:3 * L + 16], AF.Ln, T.PF[:, 10:11]), ["pva:l", "PF10"], ["SF"], 16)
@@ -337,23 +346,24 @@ def rank_program(g, core, T, topo):
         V(tt(T.ZH[:], ZA, T.pvb[:, L:L + K], OP.min), zz + ["pvb:s"], ["ZH"], K)
         V(ts(sm(0), T.SF[:, 0:16], -1.0 / math.log(4.0), OP.mult, 19.0, OP.add), ["SF"], ["h"], 16)
         V(tt(sm(2), sm(0), T.KM[:], OP.add), ["h", "KM"], ["lm"], 16)
+        V(tt(DB[:, 0:16], T.SF[:, 0:16], T.KF[:], OP.add), ["SF", "KF"], ["SFx"], 16)
+        V(ts(LU[:, 0:16], DB[:, 0:16], -1.0 / math.log(4.0), OP.mult, 0.25, OP.add), ["SFx"], ["LU0"], 16)
         V(ts(sm(1), sm(0), 15.5, OP.is_lt, -4095.0, OP.mult), ["h"], ["e"], 16)
         V(tt(sm(3), sm(2), sm(1), OP.add), ["lm", "e"], ["ly"], 16)
-        V(cp(LU[:, 0:32], sm(2, 32)), ["lm", "ly"], ["LU0"], 32)
+        V(cp(LU[:, 16:32], sm(3)), ["ly"], ["LUy"], 16)
         A(act(T.ME[:], RP[:].indirect(LU[:, 0:16]), AF.Copy), allR + ["LU0"], ["M"], K, G_R, 65.0)
-        A(act(T.YE[:], RP[:].indirect(LU[:, 16:32]), AF.Copy), allR + ["LU0"], ["Y"], K, G_R, 65.0)
-        P([mm(T.pu[:, 0:K], T.WE[:], T.ME[:], True, False), mm(T.pu[:, 0:K], T.WO[:], T.ME[:], False, True)], ["WE", "WO", "M"], ["pu:u"], 2 * K)
-        P([mm(T.py[:, 0:16], T.EALL[:, i * 128:(i + 1) * 128], T.YE[:, i:K:16], i == 0, i == 15) for i in range(16)], ["EALL", "Y"], ["py:y"], 16 * 64)
-        V(tt(DA[:, 0:K], T.DIAG[:, 0:K], T.pu[:, 0:K], OP.mult), ["DIAG", "pu:u"], ["DA"], K)
-        V(scan(DB[:, 0:K], T.RESET[:, 0:K], DA[:, 0:K], OP.add), ["RESET", "DA"], ["DB"], K)
-        V(cp(sm(4), DB[:, 15:K:16]), ["DB"], ["uv"], 16)
+        A(act(T.YE[:], RP[:].indirect(LU[:, 16:32]), AF.Copy), allR + ["LUy"], ["Y"], K, G_R, 65.0)
+        P([mm(T.pu[:, 0:16], T.BO[:], T.ONES[:, 0:16], True, False)], ["BO", "ONES"], ["pu:u"], 64)
+        P([mm(T.pu[:, 0:16], T.WALL[:, i * 128:(i + 1) * 128], T.ME[:, i:K:16], False, i == 15) for i in range(16)], ["WALL", "M"], ["pu:u"], 16 * 64)
+        P([mm(T.pva[:, 400:416], T.EALL[:, i * 128:(i + 1) * 128], T.YE[:, i:K:16], i == 0, i == 15) for i in range(16)], ["EALL", "Y"], ["pva:y"], 16 * 64)
+        V(cp(sm(4), T.pu[:, 0:16]), ["pu:u"], ["uv"], 16)
         V(ts(sm(6), sm(4), 4095, OP.bitwise_and), ["uv"], ["uvm"], 16)
-        V(cp(sm(5), T.py[:, 0:16]), ["py:y"], ["vy"], 16)
+        V(cp(sm(5), T.pva[:, 400:416]), ["pva:y"], ["vy"], 16)
         u, vv = sm(6), sm(5)
-        V(ts(sm(8), u, 32.0, OP.add), ["uvm"], ["u32"], 16)
-        V(tt(T.SF[:, 16:32], u, sm(8), OP.mult), ["uvm", "u32"], ["yq"], 16)
+        V(tt(T.SF[:, 16:32], u, u, OP.mult), ["uvm"], ["yq"], 16)
         V(ts(sm(9), T.SF[:, 16:32], 1.0 / 32.0, OP.mult, T.AC[:], OP.add), ["yq", "AC"], ["jf"], 16)
-        V(ts(sm(11), u, 31, OP.bitwise_and), ["uvm"], ["a31"], 16)
+        V(ts(sm(8), u, 16.0, OP.add), ["uvm"], ["u32"], 16)
+        V(ts(sm(11), sm(8), 31, OP.bitwise_and), ["u32"], ["a31"], 16)
         V(ts(sm(12), sm(9), 255, OP.bitwise_and), ["jf"], ["j"], 16)
         V(tt(sm(13), sm(11), T.K32[:], OP.add), ["a31", "K32"], ["a"], 16)
         V(cp(LU[:, 32:64], sm(12, 32)), ["j", "a"], ["LU1"], 32)
@@ -362,8 +372,7 @@ def rank_program(g, core, T, topo):
         V(ts(sm(17), sm(0), 256.0, OP.mult), ["h"], ["h256"], 16)
         V(tt(sm(18), sm(17), T.KT[:], OP.add), ["h256", "KT"], ["d0"], 16)
         V(ts(sm(14), vv, 3, OP.bitwise_and), ["vy"], ["v3"], 16)
-        V(tt(sm(15), sm(14), T.HD[:], OP.mult), ["v3", "HD"], ["vh"], 16)
-        V(ts(sm(16), sm(15), 0.5, OP.is_gt), ["vh"], ["pa"], 16)
+        V(tt(sm(16), sm(14), T.HD[:], OP.min), ["v3", "HD"], ["pa"], 16)
         V(tt(sm(27), sm(0), sm(16), OP.mult), ["h", "pa"], ["cd"], 16)
         V(scan(T.ML[:], T.RESET[:, 0:K], T.MD[:], OP.add), ["RESET", "MD"], ["ML"], K, .5)
         V(tt(sm(20), T.ML[:, 15:K:16], sm(16), OP.mult), ["ML", "pa"], ["mc"], 16)
@@ -376,7 +385,7 @@ def rank_program(g, core, T, topo):
         P([mm(T.pz[:, K:2 * K], T.IDM[:], T.YE[:], True, False), mm(T.pz[:, K:2 * K], T.NID[:], T.ZH[:], False, True)], ["IDM", "NID", "Y", "ZH"], ["pz:d"], 2 * K)
         OZ, oz = T.OZ[:, o0:o0 + K], "OZ%d" % par
         A(act(OZ, T.pz[:, K:2 * K], AF.Abs), ["pz:d"], [oz], K)
-        for qd in range(8):
+        for qd in range(8 - NDP):
             bk = bank()
             for i in range(2):
                 r = qd * 2 + i
@@ -385,39 +394,34 @@ def rank_program(g, core, T, topo):
             if qd == 0:
                 A(act(T.S8[:], T[bk][:, 0:K], AF.Identity, T.PF[:, 16 + t:17 + t]), [bk + ":0", "PF%d" % (16 + t)], ["S8"], K)
             A(act(T.WR[:, qd * 512:(qd + 1) * 512], T[bk][:], AF.Copy), [bk + ":0", bk + ":1"], ["WR%d" % qd], 512)
-        for c in range(CH):
-            cs, oc, nc = slice(c * L, c * L + L), slice(o0 + c * L, o0 + c * L + L), slice(r0 + K + c * L, r0 + K + c * L + L)
-            ck = ":%d" % c
-            c8 = 8 * c
-
-            def ls(x):
-                return LU[:, 64 + 16 * x + c8:64 + 16 * x + c8 + 8]
-            V(tt(T.AB[:, cs], T.T2[:].indirect(ls(1)), BB[:, cs], OP.mult), ["T2", bbk, "LU2"], ["AB" + ck], L, G_R)
-            V(tt(T.AD[:, cs], T.PC[:, 0:K * (t + 2)].indirect(ls(2)), T.AB[:, cs], OP.max), ["PC%d" % x for x in range(t + 2)] + ["AB" + ck, "LU2"], ["AD" + ck], L, G_R)
-            V(tt(T.QQ[:, cs], T.WR[:].indirect(ls(0)), T.AD[:, cs], OP.max), ["WR%d" % x for x in range(8)] + ["AD" + ck, "LU2"], ["Q" + ck], L, G_R)
-            V(ts(T.SI[:, cs], T.QQ[:, cs], 8191, OP.bitwise_and), ["Q" + ck], ["SI" + ck], L)
-            if last:
-                V(cp(T.YSF[:, cs], T.SI[:, cs]), ["SI" + ck], ["YSF" + ck], L)
-                D("S", dma("S", T.ys[:, cs], T.YSF[:, cs]), ["YSF" + ck], [])
-                if c == 0:
-                    D("S", dma("S", T.yz[:], OZ), [oz], [])
-                continue
-            ou, oh, ol = ["%s%d:%d" % (x, par, c) for x in ("OU", "OH", "OL")]
-            V(cp(T.OU[:, oc], T.SI[:, cs]), ["SI" + ck], [ou], L)
-            send([(T.SU[:, nc], T.OU[:, oc]), (T.SZ[:, nc], T.OZ[:, oc])], t + 1, c, "a", [ou, oz], ["SU%d:%d" % (t + 1, c), "ZZ%d:%d" % (t + 1, c)])
-            px = T.pva[:, cs] if c == 0 else T.pvb[:, 0:L]
-            kx = "pva:v" if c == 0 else "pvb:v"
-            V(cp(px, T.SI[:, cs]), ["SI" + ck], [kx], L)
-            A(act(T.OH[:, oc], px, AF.Copy), [kx], [oh], L)
-            V(tt(T.OL[:, oc], px, T.OH[:, oc], OP.subtract), [kx, oh], [ol], L)
-            send([(T.SH[:, nc], T.OH[:, oc]), (T.SL[:, nc], T.OL[:, oc])], t + 1, c, "b", [oh, ol], ["HI%d:%d" % (t + 1, c), "LO%d:%d" % (t + 1, c)])
-        if not last:
+        if NDP:
+            DS([dma("S", T.ER[:, 0:16, :], T.WR[:, 0:K]), dma("S", T.ER[:, 16:32, :], T.WR[:, 0:K])], ["WR0"], ["ER"], 2300.0)
+            DS([dma("S", T.WR[:, r * K:(r + 1) * K], T.ER[:, r:r + 16, :]) for r in range(16 - 2 * NDP, 16)], ["ER"], ["WR%d" % x for x in range(8 - NDP, 8)], 2000.0 + 500.0 * 2 * NDP)
+        V(tt(T.AB[:], T.T2[:].indirect(LU[:, 80:96]), BB[:], OP.mult), ["T2", bbk, "LU2"], ["AB"], K, G_R)
+        V(tt(T.AD[:], T.PC[:, 0:K * (t + 2)].indirect(LU[:, 96:112]), T.AB[:], OP.max), ["PC%d" % x for x in range(t + 2)] + ["AB", "LU2"], ["AD"], K, G_R)
+        V(tt(T.QQ[:], T.WR[:].indirect(LU[:, 64:80]), T.AD[:], OP.max), ["WR%d" % x for x in range(8)] + ["AD", "LU2"], ["Q"], K, G_R)
+        V(ts(T.SI[:], T.QQ[:], 8191, OP.bitwise_and), ["Q"], ["SI"], K)
+        if last:
+            V(cp(T.YSF[:], T.SI[:]), ["SI"], ["YSF"], K)
+            D("S", dma("S", T.ys[:], T.YSF[:]), ["YSF"], [])
+            D("S", dma("S", T.yz[:], OZ), [oz], [])
+        else:
+            ou = "OU%d" % par
+            V(cp(T.OU[:, o0:o0 + K], T.SI[:]), ["SI"], [ou], K)
+            send([(T.SU[:, r0 + K:r0 + 2 * K], T.OU[:, o0:o0 + K]), (T.SZ[:, r0 + K:r0 + 2 * K], OZ)], t + 1, 0, "a", [ou, oz],
+                 [x % (t + 1) for x in ("SU%d:0", "SU%d:1", "ZZ%d:0", "ZZ%d:1")])
+            oc, nc, px = slice(o0, o0 + K), slice(r0 + K, r0 + 2 * K), T.pva[:, L:L + K]
+            oh, ol = "OH%d" % par, "OL%d" % par
+            V(cp(px, T.SI[:]), ["SI"], ["pva:x"], K)
+            A(act(T.OH[:, oc], px, AF.Copy), ["pva:x"], [oh], K)
+            V(tt(T.OL[:, oc], px, T.OH[:, oc], OP.subtract), ["pva:x", oh], [ol], K)
+            send([(T.SH[:, nc], T.OH[:, oc]), (T.SL[:, nc], T.OL[:, oc])], t + 1, 0, "b", [oh, ol], [x % (t + 1) for x in ("HI%d:0", "HI%d:1", "LO%d:0", "LO%d:1")])
             V(tt(T.XS[:], T.XT[:].indirect(LU[:, 48:64]), T.ME[:], OP.add), ["XT", "LU1", "M"], ["XS"], K, G_R)
             V(ts(T.XD[:], T.XS[:], 1, OP.arith_shift_right), ["XS"], ["XD"], K)
             V(cp(T.XT[:].indirect(LU[:, 48:64]), T.XD[:]), ["XD", "LU1"], ["XT"], K, 4)
-            P([mm(T.pm[:, 0:16], T.ONES[:], T.HD[:], True, True)], ["ONES", "HD"], ["pm:a"], 64)
-            V(lambda: v.tensor_reduce(out=T.AR[:], in_=T.pm[:, 0:16], axis=AxisListType.X, op=OP.add), ["pm:a"], ["AR"], 16)
-            V(ts(T.AC[:], T.AR[:], -1.0, OP.mult, 2048.0 - 0.4375, OP.add), ["AR"], ["AC"], 1)
+            P([mm(T.pm[:, 0:16], T.ONES[:, 0:128], T.HD[:], True, True)], ["ONES", "HD"], ["pm:a"], 64)
+            A(lambda: s.activation(out=T.ACT[:], in_=T.pm[:, 0:16], func=AF.Copy, accum_out=T.AR[:]), ["pm:a"], ["AR"], 16, 1.0, 140.0)
+            A(lambda: s.activation(out=T.AC[:], in_=T.AR[:], func=AF.Identity, bias=T.PF[:, 12:13], scale=-1.0), ["AR", "PF12"], ["AC"], 1)
         pk, PD = ("PL", T.PL[:]) if last else ("PC%d" % (t + 2), T.PC[:, K * (t + 2):K * (t + 3)])
         V(tt(PD, T.T1[:].indirect(LU[:, 112:128]), T.S8[:], OP.mult), ["T1", "S8", "LU2"], [pk], K, G_R)
         V(tt(CT, CT, PD, OP.max), ["pm:c", pk], ["pm:c"], K)

import math
from concourse.bass import DstId, RemoteDMATransfer
from concourse.mybir import AluOpType as OP, AxisListType, ActivationFunctionType as AF

RO = 6
CH, L = 2, 128
K = CH * L
NDP = 4
PXN = 32
PIECES = [(0, 64, "A"), (64, 32, "V"), (96, 32, "V"), (128, 64, "A"), (192, 64, "A")]
CHUNKS = [(0, 128, 0), (128, 64, 0), (192, 64, 0)]
SIGNQ = 1
DELTA = 300.0

SCRATCH = {
    "XT": ("sbuf", [128, 8192], "bfloat16"), "PC": ("sbuf", [128, 2048], "float32"),
    "NB0": ("sbuf", [128, 256], "bfloat16"), "NB1": ("sbuf", [128, 256], "bfloat16"),
    "EALL": ("sbuf", [128, 2048], "bfloat16"), "RALL": ("sbuf", [128, 2048], "bfloat16"), "RESET": ("sbuf", [128, 2048], "bfloat16"),
    "BO": ("sbuf", [128, 128], "bfloat16"), "IDM": ("sbuf", [128, 128], "bfloat16"), "NID": ("sbuf", [128, 128], "bfloat16"),
    "ONES": ("sbuf", [128, 256], "bfloat16"), "DIAG": ("sbuf", [128, 256], "bfloat16"), "WALL": ("sbuf", [128, 2048], "float16"),
    "ACT": ("sbuf", [128, 16], "float32"), "KF": ("sbuf", [128, 16], "float32"), "T1": ("sbuf", [128, 16], "bfloat16"), "T2": ("sbuf", [128, 32], "bfloat16"),
    "NV": ("sbuf", [128, 128], "float32"), "SEL": ("sbuf", [128, 128], "bfloat16"),
    "IO1": ("sbuf", [128, 2048], "bfloat16"), "IO2": ("sbuf", [128, 128], "bfloat16"), "IO3": ("sbuf", [128, 256], "bfloat16"),
    "IO4": ("sbuf", [128, 128], "bfloat16"), "IO5": ("sbuf", [128, 128], "int32"), "RL1": ("sbuf", [128, 128], "int32"),
    "RL2": ("sbuf", [128, 128], "int32"), "RLU": ("sbuf", [128, 128], "uint16"), "K0": ("sbuf", [128, 16], "int32"),
    "KT": ("sbuf", [128, 16], "int32"), "KM": ("sbuf", [128, 16], "int32"), "K32": ("sbuf", [128, 16], "int32"),
    "PI": ("sbuf", [128, 8], "int32"), "PF": ("sbuf", [128, 24], "float32"), "F4": ("sbuf", [128, 16], "float32"),
    "Z0": ("sbuf", [128, 16], "float32"), "PWS": ("sbuf", [128, 16], "float32"), "PWM": ("sbuf", [128, 16], "float32"),
    "PW": ("sbuf", [128, 1], "float32"), "WI": ("sbuf", [128, 8], "int32"), "WF": ("sbuf", [128, 8], "float32"),
    "LNI": ("sbuf", [128, 256], "int32"), "LNB": ("sbuf", [128, 256], "bfloat16"), "PCM": ("sbuf", [128, 256], "bfloat16"),
    "STI": ("sbuf", [128, 256], "int32"), "BAI": ("sbuf", [128, 256], "int32"), "COI": ("sbuf", [128, 256], "int32"),
    "HD": ("sbuf", [128, 16], "bfloat16"), "AR": ("sbuf", [128, 1], "float32"), "AC": ("sbuf", [128, 1], "float32"),
    "FI": ("sbuf", [128, 256], "int32"), "FJ": ("sbuf", [128, 256], "int32"), "FC": ("sbuf", [128, 256], "float32"),
    "FN": ("sbuf", [128, 256], "int32"), "FM": ("sbuf", [128, 256], "int32"), "FL": ("sbuf", [128, 256], "float32"),
    "ER": ("dram", [8, 32, 256], "float32"), "YSF": ("sbuf", [128, 256], "float32"),
    "RP": ("sbuf", [128, 8192], "bfloat16"),
    "GE": ("sbuf", [128, 4096], "bfloat16"), "WR": ("sbuf", [128, 4096], "float32"), "HP": ("sbuf", [128, 256], "bfloat16"),
    "ZH": ("sbuf", [128, 256], "bfloat16"), "DA": ("sbuf", [128, 512], "float32"), "DB": ("sbuf", [128, 512], "float32"),
    "SM": ("sbuf", [128, 512], "int32"), "SF": ("sbuf", [128, 32], "float32"), "LU": ("sbuf", [128, 128], "uint16"),
    "ME": ("sbuf", [128, 256], "bfloat16"), "YE": ("sbuf", [128, 256], "bfloat16"), "XS": ("sbuf", [128, 256], "int32"),
    "XD": ("sbuf", [128, 256], "int32"), "AB": ("sbuf", [128, 256], "float32"), "AD": ("sbuf", [128, 256], "float32"),
    "QQ": ("sbuf", [128, 256], "int32"), "SI": ("sbuf", [128, 256], "int32"), "S8": ("sbuf", [128, 256], "float32"),
    "MD": ("sbuf", [128, 256], "bfloat16"), "ML": ("sbuf", [128, 256], "bfloat16"), "PL": ("sbuf", [128, 256], "float32"),
    "pz": ("psum", [128, 512], "float32"), "pva": ("psum", [128, 512], "float32"), "pvb": ("psum", [128, 512], "float32"),
    "pu": ("psum", [128, 512], "float32"), "pm": ("psum", [128, 512], "float32"), "pr0": ("psum", [128, 512], "float32"),
    "pr1": ("psum", [128, 512], "float32"), "pr2": ("psum", [128, 512], "float32"),
}
for _d in range(4):
    SCRATCH["BB%d" % _d] = ("sbuf", [128, 256], "float32")
for _n, _ty in (("U", "uint16"), ("Z", "bfloat16"), ("H", "bfloat16"), ("L", "bfloat16")):
    SCRATCH["S" + _n] = ("sbuf", [128, RO * 256], _ty)
    SCRATCH["O" + _n] = ("sbuf", [128, 2 * 256], _ty)

SEMAPHORES = ["cV", "cA", "cT", "cG", "loc"] + ["lo%d" % i for i in range(20)] + ["dm%d" % i for i in range(24)] + ["bs%d" % d for d in (1, 2, 3)] + \
             ["ar%d%d%s" % (t, c, s) for t in range(1, RO) for c in range(CH) for s in "ab"]

ORDER = {}
BONUS = {"IO": -2000.0, "HP": 8000.0, "XS": -20000.0, "OL": -8000.0, "pa": -2000.0, "SU": -2000.0, "pr": -20000.0, "NB": -20000.0, "pm": 8000.0,
         "uv": -8000.0, "e": -20000.0, "HI": 2000.0, "XT": -20000.0, "pz": -20000.0}
CYC = 0.83 * 1.2
G_R = 1.55


def make_order(ops, deps, log=None):
    n = len(ops)
    succ = [[] for _ in range(n)]
    for i in range(n):
        for j in deps[i]:
            succ[j].append(i)
    prio = [0.0] * n
    for i in range(n - 1, -1, -1):
        op = ops[i]
        prio[i] = op["cost"] + max([op["lat"] + prio[x] for x in succ[i]] + [0.0])
    for i in range(n):
        prio[i] += max([BONUS.get(w.split(":")[0].rstrip("0123456789"), 0.0) for w in ops[i]["w"]] + [-9e9]) if ops[i]["w"] else 0.0
    left = [len(deps[i]) for i in range(n)]
    est = [0.0] * n
    qs = ["V", "A", "T", "S", "G"]
    ready = {q: [] for q in qs}
    for i in range(n):
        if left[i] == 0:
            ready[ops[i]["q"]].append(i)
    qt = {q: 0.0 for q in qs}
    order = []
    while len(order) < n:
        best = None
        for q in qs:
            if not ready[q]:
                continue
            m0 = max(qt[q], min([est[i] for i in ready[q]]))
            if best is None or m0 < best[0]:
                best = (m0, q)
        m0, q = best
        i = max([x for x in ready[q] if est[x] <= m0 + DELTA], key=lambda x: (prio[x], -x))
        st = max(qt[q], est[i])
        ready[q].remove(i)
        qt[q] = st + ops[i]["cost"]
        order.append(i)
        if log is not None:
            log.append((i, st))
        for x in succ[i]:
            cross = ops[x]["q"] != q or deps[x][i]
            est[x] = max(est[x], qt[q] + (ops[i]["lat"] if cross else 0.0))
            left[x] -= 1
            if left[x] == 0:
                ready[ops[x]["q"]].append(x)
    return order, max(qt.values())


def rank_program(g, core, T, topo):
    rank = T.rank_of(core)
    if rank is None:
        return
    n_ranks = len(T.cores)
    ops = []
    eng = {"V": g.vector, "A": g.scalar, "T": g.tensor, "S": g.sync, "G": g}

    def add(q, fns, reads, writes, cost, lat=60.0, kind="c", sem=None, amount=0, banks=()):
        ops.append({"q": q, "fns": fns if isinstance(fns, list) else [fns], "r": list(reads), "w": list(writes), "cost": cost,
                    "lat": lat, "kind": kind, "sem": sem, "amount": amount, "banks": list(banks)})

    def vc(n, rate=1.0):
        return max(64.0, n * rate) * CYC

    def isps(keys):
        return sorted(set(k.split(":")[0] for k in keys if k.startswith("p")))

    def V(fn, reads, writes, n, rate=1.0):
        add("V", fn, reads, writes, vc(n, rate), banks=isps(list(reads) + list(writes)))

    def A(fn, reads, writes, n, rate=1.0, extra=0.0):
        add("A", fn, reads, writes, vc(n, rate) + extra, banks=isps(list(reads) + list(writes)))

    def P(fns, reads, writes, cyc):
        add("T", fns, reads, writes, cyc * 0.8, banks=isps(list(reads) + list(writes)))

    def G(fn, reads, writes, n):
        add("G", fn, reads, writes, 130 + 2 * n * CYC)

    ndma = [0]

    def D(q, fn, reads, writes, lat=2500.0):
        add(q, fn, reads, writes, 60.0, lat, "d", "dm%d" % ndma[0], 16)
        ndma[0] += 1

    def DS(fns, reads, writes, lat):
        add("S", fns, reads, writes, 60.0 * len(fns), lat, "d", "dm%d" % ndma[0], 16 * len(fns))
        ndma[0] += 1

    v, s, te = g.vector, g.scalar, g.tensor

    def tt(o, a, b, op):
        return lambda: v.tensor_tensor(out=o, in0=a, in1=b, op=op)

    def ts(o, a, s1, op0, s2=None, op1=None):
        if op1 is None:
            return lambda: v.tensor_scalar(out=o, in0=a, scalar1=s1, scalar2=None, op0=op0)
        return lambda: v.tensor_scalar(out=o, in0=a, scalar1=s1, scalar2=s2, op0=op0, op1=op1)

    def cp(o, a):
        return lambda: v.tensor_copy(out=o, in_=a)

    def scan(o, d0, d1, op1, ini=0.0):
        return lambda: v.tensor_tensor_scan(out=o, data0=d0, data1=d1, initial=ini, op0=OP.mult, op1=op1)

    def act(o, a, f, bias=0.0):
        return lambda: s.activation(out=o, in_=a, func=f, bias=bias)

    def mm(o, lh, rh, st, sp):
        return lambda: te.matmul(out=o, lhsT=lh, rhs=rh, start=st, stop=sp)

    def ms(o, x):
        return lambda: v.memset(o, x)

    def io(o, pat, ch, flag=True, base=0):
        if flag:
            return lambda: g.iota(o, pattern=pat, base=base, channel_multiplier=ch, allow_small_or_imprecise_dtypes=True)
        return lambda: g.iota(o, pattern=pat, base=base, channel_multiplier=ch)

    def dma(q, o, a):
        return lambda: eng[q].dma_start(out=o, in_=a)

    V(ms(T.PF[:, 9:10], 0.5), [], ["PF9"], 1)
    V(ms(T.PF[:, 10:11], 64.0), [], ["PF10"], 1)
    V(ms(T.PF[:, 11:12], 8.5), [], ["PF11"], 1)
    V(ms(T.PF[:, 12:13], 2040.0 - 0.4375), [], ["PF12"], 1)
    for t in range(RO):
        V(ms(T.PF[:, 16 + t:17 + t], 8192.0 * (t + 2)), [], ["PF%d" % (16 + t)], 1)

    D("S", dma("S", T.XT[:], T.xt[:]), [], ["XT"], 9000.0)
    D("A", dma("A", T.STI[:], T.stk[:]), [], ["STI"])
    D("A", dma("A", T.SZ[:, 0:256], T.z[:]), [], ["ZZ0:0", "ZZ0:1"])
    D("S", dma("S", T.WI[:, 0:1], T.w[:]), [], ["WI"])
    D("S", dma("S", T.BAI[:], T.bas[:]), [], ["BAI"])
    D("A", dma("A", T.LNI[0:8, :], T.ln[:]), [], ["LNI"])
    D("S", dma("S", T.COI[:], T.con[:]), [], ["COI"])

    G(io(T.PI[:, 0:1], [[0, 1]], 1, False), [], ["PI0"], 1)
    V(ts(T.PI[:, 1:2], T.PI[:, 0:1], 15, OP.bitwise_and), ["PI0"], ["PI1"], 1)
    V(ts(T.PI[:, 2:3], T.PI[:, 0:1], 112, OP.bitwise_and), ["PI0"], ["PI2"], 1)
    V(cp(T.PF[:, 0:3], T.PI[:, 0:3]), ["PI0", "PI1", "PI2"], ["PF0"], 3)
    pf, pmf, p16 = T.PF[:, 0:1], T.PF[:, 1:2], T.PF[:, 2:3]
    V(ts(T.PF[:, 3:4], pmf, -1.0, OP.mult, 16.0, OP.add), ["PF0"], ["PF3"], 1)
    V(ts(T.PF[:, 4:5], pmf, -1.0, OP.mult, 15.0, OP.add), ["PF0"], ["PF4"], 1)
    V(ts(T.PF[:, 5:6], pf, 16.0, OP.mult), ["PF0"], ["PF5"], 1)
    V(ts(T.PF[:, 6:7], pmf, 256.0, OP.mult), ["PF0"], ["PF6"], 1)
    V(ts(T.PF[:, 7:8], pmf, 15.5 - 4 * SIGNQ, OP.is_gt, -7.5, OP.mult), ["PF0"], ["PF7"], 1)
    V(ts(T.PF[:, 8:9], T.PF[:, 7:8], 8.5, OP.add), ["PF7"], ["PF8"], 1)
    G(io(T.IO4[:], [[1, 128]], 0), [], ["IO4"], 128)
    G(io(T.RL1[:], [[1, 16], [0, 8]], 1, False), [], ["RL1"], 128)
    G(io(T.IO5[:], [[0, 16], [16, 8]], 0, False), [], ["IO5"], 128)
    G(io(T.IO3[:], [[0, 16], [1, 16]], 0), [], ["IO3"], 256)
    G(io(T.IO1[:], [[-1, 16], [1, 128]], 0), [], ["IO1"], 2048)
    G(io(T.IO2[:], [[16, 8], [0, 16]], 0), [], ["IO2"], 128)
    G(io(T.K0[:], [[16, 16]], 0, False), [], ["K0"], 16)
    G(io(T.NV[:], [[8192, 8], [256, 16]], 0, True, -256), [], ["NV"], 128)
    V(ms(T.NV[:, 0:128:16], 0.0), [], ["NV"], 8)
    V(ts(T.IDM[:], T.IO4[:], pf, OP.is_equal), ["IO4", "PF0"], ["IDM"], 128, .5)
    V(ts(T.NID[:], T.IDM[:], -1.0, OP.mult), ["IDM"], ["NID"], 128, .5)
    V(cp(T.SU[:, 0:K], T.STI[:]), ["STI"], ["SU0:0", "SU0:1"], K)
    V(cp(T.SH[:, 0:K], T.STI[:]), ["STI"], ["HI0:0", "HI0:1"], K)
    V(tt(T.SL[:, 0:K], T.STI[:], T.SH[:, 0:K], OP.subtract), ["STI", "HI0:0", "HI0:1"], ["LO0:0", "LO0:1"], K, 2)
    V(ts(T.RL2[:], T.RL1[:], 15, OP.bitwise_and), ["RL1"], ["RL2"], 128)
    V(tt(T.RL1[:], T.RL2[:], T.IO5[:], OP.add), ["RL2", "IO5"], ["RL1"], 128, 2)
    V(cp(T.RLU[:], T.RL1[:]), ["RL1"], ["RLU"], 128)
    A(act(T.RALL[:], T.IDM[:, 0:128].indirect(T.RLU[:, 0:128]), AF.Copy), ["IDM", "RLU"], ["RALL"], 2048, G_R)
    V(ts(T.EALL[:], T.IO1[:], p16, OP.is_equal), ["IO1", "PF0"], ["EALL"], 2048, .5)
    V(ms(T.RESET[:], 1.0), [], ["RESET"], 2048, .5)
    V(ms(T.RESET[:, 0:2048:16], 0.0), [], ["RESET"], 128, .5)
    V(ts(T.DIAG[:], T.IO3[:], pmf, OP.is_equal), ["IO3", "PF0"], ["DIAG"], 256, .5)
    V(ts(T.T1[:], T.IO4[:, 0:16], pmf, OP.is_gt), ["IO4", "PF0"], ["T1"], 16)
    V(ts(T.T2[:], T.IO4[:, 0:32], T.PF[:, 3:4], OP.is_ge), ["IO4", "PF3"], ["T2"], 32)
    V(ms(T.T2[:, 16:32], 0.0), [], ["T2"], 16)
    V(ts(T.BO[:], T.IO2[:], p16, OP.is_equal), ["IO2", "PF0"], ["BO"], 128, .5)
    V(ms(T.ONES[:], 1.0), [], ["ONES"], 256, .5)
    V(ts(T.KT[:], T.K0[:], pmf, OP.add), ["K0", "PF0"], ["KT"], 16)
    V(ts(T.KM[:], T.KT[:], 16.0, OP.mult, 4095.0, OP.add), ["KT"], ["KM"], 16)
    V(ts(T.K32[:], T.KT[:], 32.0, OP.mult), ["KT"], ["K32"], 16)
    V(ts(T.KF[:], T.KT[:], -16.0 * math.log(4.0), OP.mult, -(4095.0 + 19.0) * math.log(4.0), OP.add), ["KT"], ["KF"], 16)
    V(ms(T.F4[:], 4.0), [], ["F4"], 16)
    V(ms(T.Z0[:], 0.0), [], ["Z0"], 16)
    V(scan(T.PWS[:], T.F4[:], T.Z0[:], OP.add, 64.0), ["F4", "Z0"], ["PWS"], 16)
    V(ms(T.PWS[:, 15:16], 0.0), [], ["PWS"], 1)
    V(ts(T.PWM[:], T.IO4[:, 0:16], T.PF[:, 4:5], OP.is_equal), ["IO4", "PF4"], ["PWM"], 16)
    V(tt(T.PWM[:], T.PWM[:], T.PWS[:], OP.mult), ["PWM", "PWS"], ["PWM"], 16)
    V(lambda: v.tensor_reduce(out=T.PW[:], in_=T.PWM[:], axis=AxisListType.X, op=OP.add), ["PWM"], ["PW"], 16)
    V(cp(T.WF[:, 0:1], T.WI[:, 0:1]), ["WI"], ["WF"], 1)
    V(ts(T.WALL[:], T.EALL[:], T.WF[:, 0:1], OP.mult), ["EALL", "WF"], ["WALL"], 2048, .5)
    V(ms(T.AC[:], -8.4375), [], ["AC"], 1)
    V(ts(T.BB0[:], T.BAI[:], 8192.0, OP.add), ["BAI"], ["BB0"], 256)

    def remote(pairs, dst, sem, lsem):
        es = topo.engines(core, dst)
        per = len(es) // len(pairs)
        rid, pid, _ = topo.addr(dst)
        tr = []
        for i, (o, a) in enumerate(pairs):
            m = sum(1 << e for e in es[i * per:(i + 1) * per])
            tr.append(RemoteDMATransfer(dst_ids=[DstId(rid=rid, pnc=pid)], dma_engine_mask=m, remote_sem=T.sem[sem], srcs=[a], dsts=[o], alu_op=0))
        return lambda: g.remote_dma_fused(tr, local_sem=T.sem[lsem])

    n_eng = len(topo.engines(core, T.cores[(rank + 1) % n_ranks]))
    for d in (1, 2, 3):
        dst = T.cores[(rank + d) % n_ranks]
        add("G", remote([(T["BB%d" % d][:], T.BB0[:])], dst, "bs%d" % d, "loc"), ["BB0"], ["BB%d" % d], 1000.0, 4000.0, "r", "bs%d" % d, n_eng)
    V(cp(T.LNB[0:8, :], T.LNI[0:8, :]), ["LNI"], ["LNB"], 256)
    V(ts(T.SEL[0:8, :], T.IO2[0:8, :], T.PF[0:8, 5:6], OP.is_equal, 256.0, OP.mult), ["IO2", "PF5"], ["SEL"], 128)
    P([mm(T.pm[:, 0:256], T.SEL[0:8, :], T.LNB[0:8, :], True, True)], ["SEL", "LNB"], ["pm:0"], 256)
    V(ts(T.NB0[:], T.pm[:, 0:256], 7936.0, OP.add), ["pm:0"], ["NB0"], 256)
    V(ts(T.PCM[:], T.pm[:, 0:256], T.PF[:, 6:7], OP.is_gt), ["pm:0", "PF6"], ["PCM"], 256)
    V(ms(T.PC[:, 0:256], 0.0), [], ["PC0"], 256)
    V(ts(T.PL[:], T.COI[:], 8192.0, OP.add), ["COI"], ["PL"], 256)
    V(tt(T.PC[:, 256:512], T.PL[:], T.PCM[:], OP.mult), ["PL", "PCM"], ["PC1"], 256, 2)
    V(cp(T.pm[:, 256:512], T.PL[:]), ["PL"], ["pm:c"], 256)
    CT = T.pm[:, 256:512]

    rotn = [0]
    nloc = [0]
    nxt = T.cores[(rank + 1) % n_ranks]
    SM, LU, DA, DB, RP, GE = T.SM, T.LU, T.DA, T.DB, T.RP, T.GE
    pvs = [T.pva, T.pvb]

    def sm(x, w=16):
        return SM[:, x * 16:x * 16 + w]

    def bank():
        rotn[0] += 1
        return "pr%d" % (rotn[0] % 3)

    def send(pairs, t, c, part, reads, writes):
        sem, ls = "ar%d%d%s" % (t, c, part), "lo%d" % nloc[0]
        nloc[0] += 1
        add("G", remote(pairs, nxt, sem, ls), reads, writes, 1000.0, 2300.0, "r", sem, n_eng)
        ops[-1]["lsem"] = ls

    for t in range(RO):
        last = t == RO - 1
        par = t % 2
        NB, NN, nb, nn = T["NB%d" % par], T["NB%d" % (1 - par)], "NB%d" % par, "NB%d" % (1 - par)
        BB, bbk = T["BB%d" % (t % 4)], "BB%d" % (t % 4)
        r0, o0 = t * K, par * K
        su, zz, hi, lo = [["%s%d:%d" % (x, t, c) for c in range(CH)] for x in ("SU", "ZZ", "HI", "LO")]
        ZA = T.SZ[:, r0:r0 + K]
        for c in range(CH):
            P([mm(T.pz[:, c * L:c * L + L], T.IDM[:], T.SZ[:, r0 + c * L:r0 + c * L + L], True, True)], ["IDM", zz[c]], ["pz:z%d" % c], L)
        for p0, pn, pq in PIECES:
            a, rk = r0 + p0, ["R%d" % (x // 16) for x in range(p0, p0 + pn, 16)]
            rd = ["XT", su[p0 // L]]
            if pq == "A":
                A(act(RP[:, 16 * p0:16 * (p0 + pn)], T.XT[:].indirect(T.SU[:, a:a + pn]), AF.Copy), rd, rk, pn * 16, G_R, 65.0)
            else:
                V(cp(RP[:, 16 * p0:16 * (p0 + pn)], T.XT[:].indirect(T.SU[:, a:a + pn])), rd, rk, pn * 16, G_R)
        for c, (c0, cn, sq) in enumerate(CHUNKS):
            h = c0 // L
            Z = T.SZ[:, r0 + c0:r0 + c0 + cn]
            Rk = ["R%d" % (x // 16) for x in range(c0, c0 + cn, 16)]
            vrows, srows = list(range(1, 16 - 4 * sq)), list(range(16 - 4 * sq, 16))
            for qd in range(sq):
                bk = bank()
                i0 = 16 - 4 * (qd + 1)
                fns = []
                for i in range(4):
                    ob = T[bk][:, i * cn:(i + 1) * cn]
                    fns += [mm(ob, T.IDM[:], RP[:, 16 * c0 + i0 + i:16 * (c0 + cn):16], True, False), mm(ob, T.NID[:], Z, False, True)]
                P(fns, ["IDM", "NID", zz[h]] + Rk, [bk + ":s"], 8 * cn)
                A(act(GE[:, 16 * c0 + i0 * cn:16 * c0 + (i0 + 4) * cn], T[bk][:, 0:4 * cn], AF.Sign, T.PF[:, 9:10]), [bk + ":s", "PF9"],
                  ["GE%d:%d" % (i, c) for i in range(i0, i0 + 4)], 4 * cn)
            for i in vrows:
                V(tt(GE[:, 16 * c0 + i * cn:16 * c0 + (i + 1) * cn], RP[:, 16 * c0 + i:16 * (c0 + cn):16], T.pz[:, c0:c0 + cn], OP.is_ge),
                  ["pz:z%d" % h] + Rk, ["GE%d:%d" % (i, c)], cn)
            pv, kv = pvs[h], ("pva", "pvb")[h]
            seq = vrows + srows
            for x, i in enumerate(seq):
                P([mm(pv[:, c0 - h * L:c0 - h * L + cn], T.EALL[:, i * 128:(i + 1) * 128], GE[:, 16 * c0 + i * cn:16 * c0 + (i + 1) * cn], x == 0, x == len(seq) - 1)],
                  ["EALL", "GE%d:%d" % (i, c)], [kv + ":v"], cn)
            for x0 in range(c0, c0 + cn, PXN):
                V(scan(RP[:, 4096 + 16 * x0:4096 + 16 * (x0 + PXN)], T.RESET[:, 0:16 * PXN], RP[:, 16 * x0:16 * (x0 + PXN)], OP.max),
                  ["R%d" % (x // 16) for x in range(x0, x0 + PXN, 16)] + ["RESET"], ["PX:%d" % x0], 16 * PXN, .5)
            if c0 + cn == L or c0 + cn == K:
                V(ts(T.HP[:, h * L:h * L + L], pv[:, 0:L], T.PF[:, 8:9] if sq else T.PF[:, 11:12], OP.is_ge, T.PW[:], OP.mult), [kv + ":v", "PW", "PF8", "PF11"], ["HP%d" % h], L)
        allR = ["R%d" % x for x in range(16)] + ["PX:%d" % x for x in range(0, K, PXN)]
        P([mm(T.pva[:, 3 * L:3 * L + 16], T.EALL[:, i * 128:(i + 1) * 128], T.HP[:, i:K:16], i == 0, i == 15) for i in range(16)],
          ["EALL", "HP0", "HP1"], ["pva:l"], 16 * 64)
        A(act(T.SF[:, 0:16], T.pva[:, 3 * L:3 * L + 16], AF.Ln, T.PF[:, 10:11]), ["pva:l", "PF10"], ["SF"], 16)
        P([mm(T.pvb[:, L:L + K], T.BO[:], T.HP[:], True, True)], ["BO", "HP0", "HP1"], ["pvb:s"], K)
        V(tt(T.ZH[:], ZA, T.pvb[:, L:L + K], OP.min), zz + ["pvb:s"], ["ZH"], K)
        V(ts(sm(0), T.SF[:, 0:16], -1.0 / math.log(4.0), OP.mult, 19.0, OP.add), ["SF"], ["h"], 16)
        V(tt(sm(2), sm(0), T.KM[:], OP.add), ["h", "KM"], ["lm"], 16)
        V(tt(DB[:, 0:16], T.SF[:, 0:16], T.KF[:], OP.add), ["SF", "KF"], ["SFx"], 16)
        V(ts(LU[:, 0:16], DB[:, 0:16], -1.0 / math.log(4.0), OP.mult, 0.25, OP.add), ["SFx"], ["LU0"], 16)
        V(ts(sm(1), sm(0), 15.5, OP.is_lt, -4095.0, OP.mult), ["h"], ["e"], 16)
        V(tt(sm(3), sm(2), sm(1), OP.add), ["lm", "e"], ["ly"], 16)
        V(cp(LU[:, 16:32], sm(3)), ["ly"], ["LUy"], 16)
        A(act(T.ME[:], RP[:].indirect(LU[:, 0:16]), AF.Copy), allR + ["LU0"], ["M"], K, G_R, 65.0)
        A(act(T.YE[:], RP[:].indirect(LU[:, 16:32]), AF.Copy), allR + ["LUy"], ["Y"], K, G_R, 65.0)
        P([mm(T.pu[:, 0:16], T.BO[:], T.ONES[:, 0:16], True, False)], ["BO", "ONES"], ["pu:u"], 64)
        P([mm(T.pu[:, 0:16], T.WALL[:, i * 128:(i + 1) * 128], T.ME[:, i:K:16], False, i == 15) for i in range(16)], ["WALL", "M"], ["pu:u"], 16 * 64)
        P([mm(T.pva[:, 400:416], T.EALL[:, i * 128:(i + 1) * 128], T.YE[:, i:K:16], i == 0, i == 15) for i in range(16)], ["EALL", "Y"], ["pva:y"], 16 * 64)
        V(cp(sm(4), T.pu[:, 0:16]), ["pu:u"], ["uv"], 16)
        V(ts(sm(6), sm(4), 4095, OP.bitwise_and), ["uv"], ["uvm"], 16)
        V(cp(sm(5), T.pva[:, 400:416]), ["pva:y"], ["vy"], 16)
        u, vv = sm(6), sm(5)
        V(tt(T.SF[:, 16:32], u, u, OP.mult), ["uvm"], ["yq"], 16)
        V(ts(sm(9), T.SF[:, 16:32], 1.0 / 32.0, OP.mult, T.AC[:], OP.add), ["yq", "AC"], ["jf"], 16)
        V(ts(sm(8), u, 16.0, OP.add), ["uvm"], ["u32"], 16)
        V(ts(sm(11), sm(8), 31, OP.bitwise_and), ["u32"], ["a31"], 16)
        V(ts(sm(12), sm(9), 255, OP.bitwise_and), ["jf"], ["j"], 16)
        V(tt(sm(13), sm(11), T.K32[:], OP.add), ["a31", "K32"], ["a"], 16)
        V(cp(LU[:, 32:64], sm(12, 32)), ["j", "a"], ["LU1"], 32)
        V(tt(T.MD[:], NB[:].indirect(LU[:, 32:48]), T.DIAG[:, 0:K], OP.mult), [nb, "LU1", "DIAG"], ["MD"], K, G_R)
        V(ts(T.HD[:], sm(0), 15.5, OP.is_lt), ["h"], ["HD"], 16)
        V(ts(sm(17), sm(0), 256.0, OP.mult), ["h"], ["h256"], 16)
        V(tt(sm(18), sm(17), T.KT[:], OP.add), ["h256", "KT"], ["d0"], 16)
        V(ts(sm(14), vv, 3, OP.bitwise_and), ["vy"], ["v3"], 16)
        V(tt(sm(16), sm(14), T.HD[:], OP.min), ["v3", "HD"], ["pa"], 16)
        V(tt(sm(27), sm(0), sm(16), OP.mult), ["h", "pa"], ["cd"], 16)
        V(scan(T.ML[:], T.RESET[:, 0:K], T.MD[:], OP.add), ["RESET", "MD"], ["ML"], K, .5)
        V(tt(sm(20), T.ML[:, 15:K:16], sm(16), OP.mult), ["ML", "pa"], ["mc"], 16)
        V(tt(sm(21), sm(18), sm(20), OP.subtract), ["d0", "mc"], ["d"], 16)
        V(ts(sm(22), sm(20), 5, OP.arith_shift_right, 0x700, OP.bitwise_and), ["mc"], ["ver"], 16)
        V(ts(sm(24), sm(21), 4095, OP.bitwise_and), ["d"], ["lr"], 16)
        V(ts(sm(25), sm(21), 8, OP.arith_shift_right, 31, OP.bitwise_and), ["d"], ["ls"], 16)
        V(tt(sm(26), sm(22), sm(12), OP.add), ["ver", "j"], ["lp"], 16)
        V(cp(LU[:, 64:128], sm(24, 64)), ["lr", "ls", "lp", "cd"], ["LU2"], 64)
        P([mm(T.pz[:, K:2 * K], T.IDM[:], T.YE[:], True, False), mm(T.pz[:, K:2 * K], T.NID[:], T.ZH[:], False, True)], ["IDM", "NID", "Y", "ZH"], ["pz:d"], 2 * K)
        OZ, oz = T.OZ[:, o0:o0 + K], "OZ%d" % par
        A(act(OZ, T.pz[:, K:2 * K], AF.Abs), ["pz:d"], [oz], K)
        for qd in range(8 - NDP):
            bk = bank()
            for i in range(2):
                r = qd * 2 + i
                ob, lh = T[bk][:, i * K:(i + 1) * K], T.RALL[:, r * 128:(r + 1) * 128]
                P([mm(ob, lh, T.SH[:, r0:r0 + K], True, False), mm(ob, lh, T.SL[:, r0:r0 + K], False, True)], ["RALL"] + hi + lo, [bk + ":%d" % i], 2 * K)
            if qd == 0:
                A(act(T.S8[:], T[bk][:, 0:K], AF.Identity, T.PF[:, 16 + t:17 + t]), [bk + ":0", "PF%d" % (16 + t)], ["S8"], K)
            A(act(T.WR[:, qd * 512:(qd + 1) * 512], T[bk][:], AF.Copy), [bk + ":0", bk + ":1"], ["WR%d" % qd], 512)
        if NDP:
            DS([dma("S", T.ER[:, 0:16, :], T.WR[:, 0:K]), dma("S", T.ER[:, 16:32, :], T.WR[:, 0:K])], ["WR0"], ["ER"], 2300.0)
            DS([dma("S", T.WR[:, r * K:(r + 1) * K], T.ER[:, r:r + 16, :]) for r in range(16 - 2 * NDP, 16)], ["ER"], ["WR%d" % x for x in range(8 - NDP, 8)], 2000.0 + 500.0 * 2 * NDP)
        V(tt(T.AB[:], T.T2[:].indirect(LU[:, 80:96]), BB[:], OP.mult), ["T2", bbk, "LU2"], ["AB"], K, G_R)
        V(tt(T.AD[:], T.PC[:, 0:K * (t + 2)].indirect(LU[:, 96:112]), T.AB[:], OP.max), ["PC%d" % x for x in range(t + 2)] + ["AB", "LU2"], ["AD"], K, G_R)
        V(tt(T.QQ[:], T.WR[:].indirect(LU[:, 64:80]), T.AD[:], OP.max), ["WR%d" % x for x in range(8)] + ["AD", "LU2"], ["Q"], K, G_R)
        V(ts(T.SI[:], T.QQ[:], 8191, OP.bitwise_and), ["Q"], ["SI"], K)
        if last:
            V(cp(T.YSF[:], T.SI[:]), ["SI"], ["YSF"], K)
            D("S", dma("S", T.ys[:], T.YSF[:]), ["YSF"], [])
            D("S", dma("S", T.yz[:], OZ), [oz], [])
        else:
            ou = "OU%d" % par
            V(cp(T.OU[:, o0:o0 + K], T.SI[:]), ["SI"], [ou], K)
            send([(T.SU[:, r0 + K:r0 + 2 * K], T.OU[:, o0:o0 + K]), (T.SZ[:, r0 + K:r0 + 2 * K], OZ)], t + 1, 0, "a", [ou, oz],
                 [x % (t + 1) for x in ("SU%d:0", "SU%d:1", "ZZ%d:0", "ZZ%d:1")])
            oc, nc, px = slice(o0, o0 + K), slice(r0 + K, r0 + 2 * K), T.pva[:, L:L + K]
            oh, ol = "OH%d" % par, "OL%d" % par
            V(cp(px, T.SI[:]), ["SI"], ["pva:x"], K)
            A(act(T.OH[:, oc], px, AF.Copy), ["pva:x"], [oh], K)
            V(tt(T.OL[:, oc], px, T.OH[:, oc], OP.subtract), ["pva:x", oh], [ol], K)
            send([(T.SH[:, nc], T.OH[:, oc]), (T.SL[:, nc], T.OL[:, oc])], t + 1, 0, "b", [oh, ol], [x % (t + 1) for x in ("HI%d:0", "HI%d:1", "LO%d:0", "LO%d:1")])
            V(tt(T.XS[:], T.XT[:].indirect(LU[:, 48:64]), T.ME[:], OP.add), ["XT", "LU1", "M"], ["XS"], K, G_R)
            V(ts(T.XD[:], T.XS[:], 1, OP.arith_shift_right), ["XS"], ["XD"], K)
            V(cp(T.XT[:].indirect(LU[:, 48:64]), T.XD[:]), ["XD", "LU1"], ["XT"], K, 4)
            P([mm(T.pm[:, 0:16], T.ONES[:, 0:128], T.HD[:], True, True)], ["ONES", "HD"], ["pm:a"], 64)
            A(lambda: s.activation(out=T.ACT[:], in_=T.pm[:, 0:16], func=AF.Copy, accum_out=T.AR[:]), ["pm:a"], ["AR"], 16, 1.0, 140.0)
            A(lambda: s.activation(out=T.AC[:], in_=T.AR[:], func=AF.Identity, bias=T.PF[:, 12:13], scale=-1.0), ["AR", "PF12"], ["AC"], 1)
        pk, PD = ("PL", T.PL[:]) if last else ("PC%d" % (t + 2), T.PC[:, K * (t + 2):K * (t + 3)])
        V(tt(PD, T.T1[:].indirect(LU[:, 112:128]), T.S8[:], OP.mult), ["T1", "S8", "LU2"], [pk], K, G_R)
        V(tt(CT, CT, PD, OP.max), ["pm:c", pk], ["pm:c"], K)
        V(tt(NN[:], T.NV[:, 16 * (t + 2):16 * (t + 3)].indirect(LU[:, 112:128]), NB[:], OP.max), ["NV", "LU2", nb], [nn], K, G_R)
    NF, nf = T["NB%d" % (RO % 2)], "NB%d" % (RO % 2)
    V(cp(T.FI[:], CT), ["pm:c"], ["FI"], K)
    V(ts(T.FJ[:], T.FI[:], 8191, OP.bitwise_and), ["FI"], ["FJ"], K)
    V(cp(T.FC[:], T.FJ[:]), ["FJ"], ["FC"], K)
    D("S", dma("S", T.yc[:], T.FC[:]), ["FC"], [])
    V(cp(T.FN[:], NF[:]), [nf], ["FN"], K)
    V(ts(T.FM[:], T.FN[:], 8, OP.arith_shift_right, 31, OP.bitwise_and), ["FN"], ["FM"], K)
    V(ts(T.FL[:], T.FM[:], 1.0, OP.add), ["FM"], ["FL"], K)
    D("S", dma("S", T.yn[:], T.FL[0:128:16, :]), ["FL"], [])

    lastw, readers, lastb = {}, {}, {}
    N = len(ops)
    deps = [dict() for _ in range(N)]

    def dep(i, j, wait):
        if i != j:
            deps[i][j] = deps[i].get(j, False) or wait

    for i in range(N):
        op = ops[i]
        for r in op["r"]:
            if r in lastw:
                dep(i, lastw[r], True)
            readers.setdefault(r, []).append(i)
        for w in op["w"]:
            acc = op["q"] == "T" and w.startswith("pv")
            if w in lastw:
                dep(i, lastw[w], not (acc and ops[lastw[w]]["q"] == "T"))
            for j in readers.get(w, []):
                dep(i, j, True)
            lastw[w] = i
            readers[w] = []
        for b in op["banks"]:
            if b in lastb:
                dep(i, lastb[b], ops[lastb[b]]["q"] != op["q"])
            lastb[b] = i

    if "order" not in ORDER:
        ORDER["order"] = make_order(ops, deps)[0]
    order = ORDER["order"]

    CN = {"V": "cV", "A": "cA", "T": "cT", "G": "cG"}
    count = {q: 0 for q in CN}
    known = {q: {} for q in eng}
    done, clock = {}, {}
    locsum = 0
    for i in order:
        op = ops[i]
        q = op["q"]
        need = {}
        for j, wait in deps[i].items():
            if not wait:
                continue
            oj = ops[j]
            if oj["kind"] == "r" and not any(w in op["r"] or w in op["w"] for w in oj["w"]):
                sem, val, cl = oj["lsem"], oj["amount"], {}
            else:
                sem, val = done[j]
                cl = clock[j] if oj["kind"] != "r" else {}
            if known[q].get(sem, 0) >= val:
                continue
            if sem not in need or need[sem][0] < val:
                need[sem] = (val, cl)
        for sem in sorted(need):
            val, cl = need[sem]
            if any(o2 != sem and need[o2][1].get(sem, 0) >= val and not (cl.get(o2, 0) >= need[o2][0]) for o2 in need):
                continue
            eng[q].wait_ge(T.sem[sem], int(val))
        for sem in need:
            val, cl = need[sem]
            known[q][sem] = max(known[q].get(sem, 0), val)
            for s2 in cl:
                known[q][s2] = max(known[q].get(s2, 0), cl[s2])
        for f in op["fns"]:
            ins = f()
            if op["kind"] == "c":
                ins.then_inc(T.sem[CN[q]], 1)
                count[q] += 1
            elif op["kind"] == "d":
                ins.then_inc(T.sem[op["sem"]], 16)
        if op["kind"] == "c":
            done[i] = (CN[q], count[q])
        else:
            done[i] = (op["sem"], op["amount"])
            if op["kind"] == "r" and "lsem" not in op:
                locsum += n_eng
        clock[i] = dict(known[q])
        clock[i][done[i][0]] = max(clock[i].get(done[i][0], 0), done[i][1])
    for q in CN:
        if count[q]:
            g.wait_ge(T.sem[CN[q]], count[q])
    g.wait_ge(T.sem.loc, locsum)
    for op in ops:
        if op["kind"] in ("d", "r") and known["G"].get(op["sem"], 0) < op["amount"]:
            g.wait_ge(T.sem[op["sem"]], op["amount"])
        if "lsem" in op and known["G"].get(op["lsem"], 0) < n_eng:
            g.wait_ge(T.sem[op["lsem"]], n_eng)
